import numpy as np
import ml_dtypes


def mxq(x, axis, fmt="e4m3"):
    dtype, down = {"e4m3": (ml_dtypes.float8_e4m3fn, 7), "e5m2": (ml_dtypes.float8_e5m2, 14)}[fmt]
    v = np.moveaxis(np.asarray(x, np.float32).astype(ml_dtypes.bfloat16).astype(np.float64), axis, -1)
    blocks = v.reshape(v.shape[:-1] + (-1, 32))
    amax = np.abs(blocks).max(-1, keepdims=True)
    byte = np.maximum(np.where(amax > 0, np.frexp(amax)[1] - 1 + 127, 0) - down, 1)
    scale = np.exp2(byte - 127.0)
    codes = (blocks / scale).astype(np.float32).astype(dtype).astype(np.float64)
    return np.moveaxis((codes * scale).reshape(v.shape), -1, axis)


WIDE = False


def mx_kscale(k):
    if not WIDE:
        return np.ones(k)
    levels = np.array([10, -10, 5, -5, 0])
    if k % 512:
        return np.exp2(np.random.permutation(np.resize(levels, k // 32))).repeat(32)
    a = np.empty((k // 512, 16))
    for p in range(k // 512):
        a[p, :8] = np.random.permutation(np.resize(levels, 8))
        for g in range(8):
            far = levels[np.abs(levels - a[p, g]) >= 10]
            a[p, g + 8] = far[np.random.randint(len(far))]
    return np.exp2(a.ravel()).repeat(32)


def f64(x):
    return np.asarray(x).astype(np.float64)


def striped(idx):
    return np.tile(idx.reshape(-1, 16).T, (8, 1)).astype(np.uint16)


def unstriped(offs):
    return offs[:16].T.reshape(-1).astype(np.int64)


def pack_weight(w):
    k, n = w.shape
    w = f64(np.asarray(w, np.float32).astype(ml_dtypes.bfloat16)).reshape(k // 32, 32, n)
    amax = np.abs(w).max(1)
    byte = np.clip(np.where(amax > 0, np.frexp(amax)[1] - 1 + 127 - 7, 1), 1, 254)
    scaled = (w * np.exp2(127.0 - byte)[:, None, :]).reshape(k, n).astype(np.float32)
    words = np.ascontiguousarray(scaled.reshape(k // 512, 128, 4, n).transpose(0, 1, 3, 2)).astype(ml_dtypes.float8_e4m3fn).view(np.uint8)
    return words, np.ascontiguousarray(byte.astype(np.uint8).reshape(k // 512, 16, n))


def unpack_weight(words, scales):
    g, p, n, _ = words.shape
    vals = np.ascontiguousarray(words).view(ml_dtypes.float8_e4m3fn).astype(np.float64) * np.repeat(np.exp2(scales.astype(np.float64) - 127.0), 8, axis=1)[..., None]
    return vals.transpose(0, 1, 3, 2).reshape(g * 512, n)


E2M1 = np.array([0.0, 0.5, 1.0, 1.5, 2.0, 3.0, 4.0, 6.0, -0.0, -0.5, -1.0, -1.5, -2.0, -3.0, -4.0, -6.0])


def pack_fp4(w):
    k, n = w.shape
    w = f64(np.asarray(w, np.float32).astype(ml_dtypes.bfloat16)).reshape(k // 32, 32, n)
    amax = np.abs(w).max(1)
    mant, ex = np.frexp(amax / 6.0)
    byte = np.clip(np.where(amax > 0, np.where(mant > 0.5, ex, ex - 1) + 127, 1), 1, 254)
    scaled = (w * np.exp2(127.0 - byte)[:, None, :]).reshape(k, n).astype(np.float32)
    c = np.ascontiguousarray(scaled.reshape(k // 512, 128, 4, n).transpose(0, 1, 3, 2)).astype(ml_dtypes.float4_e2m1fn).view(np.uint8) & 0xF
    words = (c[..., 0::2] | (c[..., 1::2] << 4)).reshape(k // 512, 128, 2 * n)
    return np.ascontiguousarray(words), np.ascontiguousarray(byte.astype(np.uint8).reshape(k // 512, 16, n))


def unpack_fp4(words, scales):
    g, _, n = scales.shape
    words = np.ascontiguousarray(words).reshape(g, 128, n, 2)
    nib = np.empty((g, 128, n, 4), np.uint8)
    nib[..., 0::2] = words & 0xF
    nib[..., 1::2] = words >> 4
    vals = E2M1[nib] * np.repeat(np.exp2(scales.astype(np.float64) - 127.0), 8, axis=1)[..., None]
    return vals.transpose(0, 1, 3, 2).reshape(g * 512, n)


def relu(v):
    return np.maximum(v, 0.0)


K, T, S, D, V, H, N, U = 1024, 2048, 512, 2, 512, 512, 128, 1024
P = 2 ** 7


def setup_inputs():
    n = np.random.standard_normal
    s = mx_kscale(K)[:, None]
    u = mx_kscale(H)
    packed_xT = pack_weight(n((K, T)) * s)
    packed_w2 = pack_fp4(n((H, N)) / np.sqrt(H) / u[:, None])
    return {
        "x_words": packed_xT[0],
        "x_scales": packed_xT[1],
        "w1": (n((K, H)) / np.sqrt(K) / s * u).astype(np.float32),
        "w2_words": packed_w2[0],
        "w2_scales": packed_w2[1],
        "gate": np.tile(np.random.uniform(0.2, 0.6, (D, 1, V)), (1, P, 1)).astype(np.float32),
        "emb": (0.5 * n((H, U)) * u[:, None]).astype(np.float32),
        "offs": striped(np.random.permutation(T)[:S]),
        "cell": striped(np.random.permutation(U)[:S]),
        "pos1": striped(np.random.permutation(U)[:V]),
        "pos2": striped(np.random.permutation(U)[:V]),
    }


def reference(x_words, x_scales, w1, w2_words, w2_scales, gate, emb, offs, cell, pos1, pos2):
    xq = unpack_weight(x_words, x_scales)[:, unstriped(offs)]
    up = np.zeros((H, U))
    up[:, unstriped(cell)] = relu(mxq(f64(w1), 0, "e4m3").T @ xq)
    z = up + f64(emb)
    y = unpack_fp4(w2_words, w2_scales).T @ mxq(z, 0, "e4m3")
    return y[:, unstriped(pos1)] * f64(gate)[0, :1] + y[:, unstriped(pos2)] * f64(gate)[1, :1]

@@ -1,0 +1,164 @@
+from contextlib import ExitStack
+
+import concourse.mybir as mybir
+
+K, T, S, V, H, N, U = 1024, 2048, 512, 512, 512, 128, 1024
+FLOPS = 2 * K * H * S + 2 * H * N * U
+
+F32 = mybir.dt.float32
+BF16 = mybir.dt.bfloat16
+I32 = mybir.dt.int32
+U32 = mybir.dt.uint32
+U16 = mybir.dt.uint16
+U8 = mybir.dt.uint8
+FP8X4 = mybir.dt.float8_e4m3fn_x4
+FP4X4 = mybir.dt.float4_e2m1fn_x4
+RELU = mybir.ActivationFunctionType.Relu
+ADD = mybir.AluOpType.add
+MULT = mybir.AluOpType.mult
+
+P = 128
+PACK = 4
+PASSES = K // (P * PACK)
+HALF = S // 2
+QUARTER = U // 4
+
+
+def tile_picked_devox_none_p_kernel(
+    tc, x_words, x_scales, w1, w2_words, w2_scales, gate, emb, offs, cell, pos1, pos2, out
+):
+    nc = tc.nc
+    with ExitStack() as ctx:
+        keep = ctx.enter_context(tc.tile_pool(name="keep", bufs=1))
+        psum = ctx.enter_context(tc.psum_pool(name="psum", bufs=1))
+
+        def load_list(src, name):
+            tile = keep.tile([P, S // 16], U16, name=name)
+            nc.sync.dma_start(tile[:], src)
+            return tile
+
+        xs_all = keep.tile([P, T], U8, name="xs_all", align_bytes=64)
+        w2_sc = keep.tile([P, N], U8, name="w2_sc", align_bytes=64)
+        nc.vector.memset(xs_all[:].bitcast(I32), 0)
+        nc.vector.memset(w2_sc[:].bitcast(I32), 0)
+        up = [keep.tile([P, U], F32, name="up%d" % t) for t in range(PACK)]
+        for t in range(PACK):
+            nc.vector.memset(up[t][:], 0.0)
+
+        offs_sb = load_list(offs, "offs_sb")
+        cell_sb = load_list(cell, "cell_sb")
+        w1_raw = [keep.tile([P, PACK, H], F32, name="w1_raw%d" % g) for g in range(PASSES)]
+        xw_all = [keep.tile([P, T], U32, name="xw_all%d" % g) for g in range(PASSES)]
+        for g in range(PASSES):
+            rows = w1[g * P * PACK : (g + 1) * P * PACK, :]
+            nc.sync.dma_start(w1_raw[g][:], rows.rearrange("(p j) c -> p j c", j=PACK))
+            if g == 0:
+                for q in range(4):
+                    nc.sync.dma_start(
+                        xs_all[32 * q : 32 * q + 4 * PASSES, :].bitcast(I32),
+                        x_scales[:, 4 * q : 4 * q + 4, :].bitcast(I32),
+                    )
+            nc.sync.dma_start(xw_all[g][:].bitcast(I32), x_words[g].rearrange("p n t -> p (n t)").bitcast(I32))
+        emb_sb = [keep.tile([P, U], F32, name="emb_sb%d" % t) for t in range(PACK)]
+        emb_rows = emb.rearrange("(p t) c -> t p c", t=PACK)
+        for t in range(PACK):
+            nc.sync.dma_start(emb_sb[t][:], emb_rows[t])
+        w2_codes = keep.tile([P, 2 * N], U8, name="w2_codes", align_bytes=64)
+        nc.sync.dma_start(w2_codes[:].bitcast(I32), w2_words[0].bitcast(I32))
+        for q in range(4):
+            nc.sync.dma_start(w2_sc[32 * q : 32 * q + 4, :].bitcast(I32), w2_scales[0, 4 * q : 4 * q + 4, :].bitcast(I32))
+        pos_sb = [load_list(pos1, "pos1_sb"), load_list(pos2, "pos2_sb")]
+        gate_sb = [keep.tile([P, V], F32, name="gate_sb%d" % d) for d in range(2)]
+        for d in range(2):
+            nc.sync.dma_start(gate_sb[d][:], gate[d])
+
+        w1_codes = [keep.tile([P, H], U32, name="w1_codes%d" % g, align_bytes=64) for g in range(PASSES)]
+        w1_sc = [keep.tile([P, H], U8, name="w1_sc%d" % g, align_bytes=64) for g in range(PASSES)]
+        xs_pick = keep.tile([P, S], U8, name="xs_pick", align_bytes=64)
+        xw_pick = {}
+        for g in range(PASSES):
+            w1_bf = keep.tile([P, H * PACK], BF16, name="w1_bf%d" % g, align_bytes=64)
+            dst = w1_bf[:].rearrange("p (t m j) -> p m t j", t=PACK, j=PACK)
+            src = w1_raw[g][:].rearrange("p j (m t) -> p m t j", t=PACK)
+            nc.vector.tensor_copy(dst[:, :64], src[:, :64])
+            nc.scalar.copy(dst[:, 64:], src[:, 64:])
+            nc.vector.quantize_mx(w1_codes[g][:].bitcast(FP8X4), w1_sc[g][:], w1_bf[:])
+            if g == 0:
+                nc.vector.tensor_copy(xs_pick[:], xs_all[:].indirect(offs_sb[:]))
+            for a in range(2):
+                xw_pick[g, a] = keep.tile([P, HALF], U32, name="xw_pick%d_%d" % (g, a), align_bytes=64)
+            if g == 0:
+                for a in range(2):
+                    nc.vector.tensor_copy(xw_pick[g, a][:], xw_all[g][:].indirect(offs_sb[:, 16 * a : 16 * (a + 1)]))
+            else:
+                for a in range(2):
+                    nc.vector.tensor_copy(xw_pick[g, a][:], xw_all[g][:].indirect(offs_sb[:, 16 * a : 16 * (a + 1)]))
+
+        acc = {}
+        for t in range(PACK):
+            for a in range(2):
+                acc[t, a] = psum.tile([P, HALF], F32, name="acc%d_%d" % (t, a), tag="bank%d" % (2 * t + a))
+        for g in range(PASSES):
+            for t in range(PACK):
+                for a in range(2):
+                    cols = slice(t * P, (t + 1) * P)
+                    nc.tensor.matmul_mx(
+                        acc[t, a][:],
+                        lhsT=w1_codes[g][:, cols].bitcast(FP8X4),
+                        lhsT_scale=w1_sc[g][:, cols],
+                        rhs=xw_pick[g, a][:].bitcast(FP8X4),
+                        rhs_scale=xs_pick[4 * g :, a * HALF : (a + 1) * HALF],
+                        start=(g == 0),
+                        stop=(g == PASSES - 1),
+                    )
+        z_rows = [keep.tile([P, PACK, U // 2], BF16, name="z_rows%d" % b) for b in range(2)]
+        for t in range(PACK):
+            if t == 0:
+                for a in range(2):
+                    h = keep.tile([P, HALF], F32, name="h0_%d" % a)
+                    nc.scalar.activation(h[:], acc[t, a][:], RELU)
+                    nc.vector.tensor_copy(up[t][:].indirect(cell_sb[:, 16 * a : 16 * (a + 1)]), h[:])
+            else:
+                h = keep.tile([P, S], F32, name="h%d" % t)
+                for a in range(2):
+                    nc.scalar.activation(h[:, a * HALF : (a + 1) * HALF], acc[t, a][:], RELU)
+                nc.vector.tensor_copy(up[t][:].indirect(cell_sb[:]), h[:])
+            for b in range(2):
+                cols = slice(b * U // 2, (b + 1) * U // 2)
+                eng = nc.vector if t == PACK - 1 else nc.gpsimd
+                eng.tensor_tensor(z_rows[b][:, t, :], up[t][:, cols], emb_sb[t][:, cols], ADD)
+
+        y = keep.tile([P, U], F32, name="y")
+        for r in (2, 0, 3, 1):
+            z_bf = keep.tile([P, QUARTER * PACK], BF16, name="z_bf%d" % r, align_bytes=64)
+            src = z_rows[r // 2][:, :, (r % 2) * QUARTER : (r % 2 + 1) * QUARTER].rearrange("p t (c i) -> p c t i", i=4)
+            dst = z_bf[:].rearrange("p (c i t) -> p c t i", i=4, t=PACK)
+            if r < 2:
+                nc.scalar.copy(dst, src)
+            else:
+                nc.vector.tensor_copy(dst, src)
+            z_codes = keep.tile([P, QUARTER], U32, name="z_codes%d" % r, align_bytes=64)
+            z_sc = keep.tile([P, QUARTER], U8, name="z_sc%d" % r, align_bytes=64)
+            nc.vector.quantize_mx(z_codes[:].bitcast(FP8X4), z_sc[:], z_bf[:])
+            y_acc = psum.tile([P, QUARTER], F32, name="y_acc%d" % r, tag="bank%d" % r)
+            nc.tensor.matmul_mx(
+                y_acc[:],
+                lhsT=w2_codes[:].bitcast(FP4X4),
+                lhsT_scale=w2_sc[:],
+                rhs=z_codes[:].bitcast(FP8X4),
+                rhs_scale=z_sc[:],
+                start=True,
+                stop=True,
+            )
+            nc.scalar.copy(y[:, r * QUARTER : (r + 1) * QUARTER], y_acc[:])
+
+        for a in range(2):
+            cols = slice(a * V // 2, (a + 1) * V // 2)
+            part = []
+            for d in range(2):
+                prod = keep.tile([P, V // 2], F32, name="prod%d_%d" % (a, d))
+                nc.vector.tensor_tensor(prod[:], y[:].indirect(pos_sb[d][:, 16 * a : 16 * (a + 1)]), gate_sb[d][:, cols], MULT)
+                part.append(prod)
+            res = keep.tile([P, V // 2], F32, name="res%d" % a)
+            nc.vector.tensor_tensor(res[:], part[0][:], part[1][:], ADD)
+            nc.sync.dma_start(out[:, cols], res[:])

@@ -39,26 +39,27 @@ def tile_picked_devox_none_p_kernel(
 
         xs_all = keep.tile([P, T], U8, name="xs_all", align_bytes=64)
         w2_sc = keep.tile([P, N], U8, name="w2_sc", align_bytes=64)
-        nc.vector.memset(xs_all[:].bitcast(I32), 0)
+        nc.gpsimd.memset(xs_all[:].bitcast(I32), 0)
         nc.vector.memset(w2_sc[:].bitcast(I32), 0)
         up = [keep.tile([P, U], F32, name="up%d" % t) for t in range(PACK)]
         for t in range(PACK):
-            nc.vector.memset(up[t][:], 0.0)
+            (nc.vector if t < 2 else nc.gpsimd).memset(up[t][:], 0.0)
 
-        offs_sb = load_list(offs, "offs_sb")
-        cell_sb = load_list(cell, "cell_sb")
         w1_raw = [keep.tile([P, PACK, H], F32, name="w1_raw%d" % g) for g in range(PASSES)]
         xw_all = [keep.tile([P, T], U32, name="xw_all%d" % g) for g in range(PASSES)]
-        for g in range(PASSES):
-            rows = w1[g * P * PACK : (g + 1) * P * PACK, :]
-            nc.sync.dma_start(w1_raw[g][:], rows.rearrange("(p j) c -> p j c", j=PACK))
-            if g == 0:
-                for q in range(4):
-                    nc.sync.dma_start(
-                        xs_all[32 * q : 32 * q + 4 * PASSES, :].bitcast(I32),
-                        x_scales[:, 4 * q : 4 * q + 4, :].bitcast(I32),
-                    )
-            nc.sync.dma_start(xw_all[g][:].bitcast(I32), x_words[g].rearrange("p n t -> p (n t)").bitcast(I32))
+        w1_rows = w1.rearrange("(g p j) c -> g p j c", p=P, j=PACK)
+        nc.sync.dma_start(w1_raw[0][:], w1_rows[0])
+        offs_sb = load_list(offs, "offs_sb")
+        for q in range(4):
+            nc.sync.dma_start(
+                xs_all[32 * q : 32 * q + 4 * PASSES, :].bitcast(I32),
+                x_scales[:, 4 * q : 4 * q + 4, :].bitcast(I32),
+            )
+        nc.sync.dma_start(w1_raw[1][:], w1_rows[1])
+        x_rows = x_words.rearrange("g p n t -> g p (n t)").bitcast(I32)
+        nc.sync.dma_start(xw_all[0][:].bitcast(I32), x_rows[0])
+        cell_sb = load_list(cell, "cell_sb")
+        nc.sync.dma_start(xw_all[1][:].bitcast(I32), x_rows[1])
         emb_sb = [keep.tile([P, U], F32, name="emb_sb%d" % t) for t in range(PACK)]
         emb_rows = emb.rearrange("(p t) c -> t p c", t=PACK)
         for t in range(PACK):
@@ -74,73 +75,77 @@ def tile_picked_devox_none_p_kernel(
 
         w1_codes = [keep.tile([P, H], U32, name="w1_codes%d" % g, align_bytes=64) for g in range(PASSES)]
         w1_sc = [keep.tile([P, H], U8, name="w1_sc%d" % g, align_bytes=64) for g in range(PASSES)]
-        xs_pick = keep.tile([P, S], U8, name="xs_pick", align_bytes=64)
-        xw_pick = {}
         for g in range(PASSES):
             w1_bf = keep.tile([P, H * PACK], BF16, name="w1_bf%d" % g, align_bytes=64)
             dst = w1_bf[:].rearrange("p (t m j) -> p m t j", t=PACK, j=PACK)
             src = w1_raw[g][:].rearrange("p j (m t) -> p m t j", t=PACK)
-            nc.vector.tensor_copy(dst[:, :64], src[:, :64])
-            nc.scalar.copy(dst[:, 64:], src[:, 64:])
+            nc.vector.tensor_copy(dst[:, : P // 2], src[:, : P // 2])
+            nc.scalar.copy(dst[:, P // 2 :], src[:, P // 2 :])
             nc.vector.quantize_mx(w1_codes[g][:].bitcast(FP8X4), w1_sc[g][:], w1_bf[:])
-            if g == 0:
-                nc.vector.tensor_copy(xs_pick[:], xs_all[:].indirect(offs_sb[:]))
-            for a in range(2):
-                xw_pick[g, a] = keep.tile([P, HALF], U32, name="xw_pick%d_%d" % (g, a), align_bytes=64)
-            if g == 0:
-                for a in range(2):
-                    nc.vector.tensor_copy(xw_pick[g, a][:], xw_all[g][:].indirect(offs_sb[:, 16 * a : 16 * (a + 1)]))
-            else:
-                for a in range(2):
-                    nc.vector.tensor_copy(xw_pick[g, a][:], xw_all[g][:].indirect(offs_sb[:, 16 * a : 16 * (a + 1)]))
+        xs_pick = keep.tile([P, S], U8, name="xs_pick", align_bytes=64)
+        xw_pick = [keep.tile([P, S], U32, name="xw_pick%d" % g, align_bytes=64) for g in range(PASSES)]
+        nc.vector.tensor_copy(xs_pick[:], xs_all[:].indirect(offs_sb[:]))
+        nc.vector.tensor_copy(xw_pick[0][:], xw_all[0][:].indirect(offs_sb[:]))
+        for a in range(2):
+            nc.vector.tensor_copy(
+                xw_pick[1][:, a * HALF : (a + 1) * HALF], xw_all[1][:].indirect(offs_sb[:, 16 * a : 16 * (a + 1)])
+            )
 
-        acc = {}
-        for t in range(PACK):
-            for a in range(2):
-                acc[t, a] = psum.tile([P, HALF], F32, name="acc%d_%d" % (t, a), tag="bank%d" % (2 * t + a))
-        for g in range(PASSES):
-            for t in range(PACK):
-                for a in range(2):
-                    cols = slice(t * P, (t + 1) * P)
-                    nc.tensor.matmul_mx(
-                        acc[t, a][:],
-                        lhsT=w1_codes[g][:, cols].bitcast(FP8X4),
-                        lhsT_scale=w1_sc[g][:, cols],
-                        rhs=xw_pick[g, a][:].bitcast(FP8X4),
-                        rhs_scale=xs_pick[4 * g :, a * HALF : (a + 1) * HALF],
-                        start=(g == 0),
-                        stop=(g == PASSES - 1),
-                    )
-        z_rows = [keep.tile([P, PACK, U // 2], BF16, name="z_rows%d" % b) for b in range(2)]
-        for t in range(PACK):
-            if t == 0:
-                for a in range(2):
-                    h = keep.tile([P, HALF], F32, name="h0_%d" % a)
-                    nc.scalar.activation(h[:], acc[t, a][:], RELU)
-                    nc.vector.tensor_copy(up[t][:].indirect(cell_sb[:, 16 * a : 16 * (a + 1)]), h[:])
-            else:
-                h = keep.tile([P, S], F32, name="h%d" % t)
-                for a in range(2):
-                    nc.scalar.activation(h[:, a * HALF : (a + 1) * HALF], acc[t, a][:], RELU)
-                nc.vector.tensor_copy(up[t][:].indirect(cell_sb[:]), h[:])
-            for b in range(2):
-                cols = slice(b * U // 2, (b + 1) * U // 2)
+        h = [keep.tile([P, S], F32, name="h%d" % t) for t in range(PACK)]
+
+        def first_product(t, lo, hi, bank):
+            acc = psum.tile([P, hi - lo], F32, name="acc%d_%d" % (t, lo), tag="bank%d" % bank)
+            cols = slice(t * P, (t + 1) * P)
+            for g in range(PASSES):
+                nc.tensor.matmul_mx(
+                    acc[:],
+                    lhsT=w1_codes[g][:, cols].bitcast(FP8X4),
+                    lhsT_scale=w1_sc[g][:, cols],
+                    rhs=xw_pick[g][:, lo:hi].bitcast(FP8X4),
+                    rhs_scale=xs_pick[4 * g :, lo:hi],
+                    start=(g == 0),
+                    stop=(g == PASSES - 1),
+                )
+            nc.scalar.activation(h[t][:, lo:hi], acc[:], RELU)
+
+        def scatter(t, lo, hi):
+            nc.vector.tensor_copy(up[t][:].indirect(cell_sb[:, lo // 16 : hi // 16]), h[t][:, lo:hi])
+
+        for t in range(2):
+            first_product(t, 0, P, t)
+            scatter(t, 0, P)
+        for t in range(2):
+            first_product(t, P, HALF, 2 + 2 * t)
+            first_product(t, HALF, S, 3 + 2 * t)
+            scatter(t, P, S)
+        for t in range(2, PACK):
+            first_product(t, 0, S, t - 2)
+            scatter(t, 0, S)
+
+        z_pair = [[keep.tile([P, 2, U // 2], BF16, name="z_pair%d_%d" % (u, b)) for b in range(2)] for u in range(2)]
+        z_bf = [keep.tile([P, QUARTER, PACK], BF16, name="z_bf%d" % r, align_bytes=64) for r in range(4)]
+        for u in range(2):
+            for e in range(2):
+                t = 2 * u + e
                 eng = nc.vector if t == PACK - 1 else nc.gpsimd
-                eng.tensor_tensor(z_rows[b][:, t, :], up[t][:, cols], emb_sb[t][:, cols], ADD)
+                for b in range(2):
+                    cols = slice(b * U // 2, (b + 1) * U // 2)
+                    eng.tensor_tensor(z_pair[u][b][:, e, :], up[t][:, cols], emb_sb[t][:, cols], ADD)
+            for r in range(4):
+                src = z_pair[u][r // 2][:, :, (r % 2) * QUARTER : (r % 2 + 1) * QUARTER].rearrange("p e c -> p c e")
+                dst = z_bf[r][:, :, 2 * u : 2 * u + 2]
+                if u == 1 and r % 2 == 1:
+                    nc.vector.tensor_copy(dst, src)
+                else:
+                    nc.scalar.copy(dst, src)
 
         y = keep.tile([P, U], F32, name="y")
-        for r in (2, 0, 3, 1):
-            z_bf = keep.tile([P, QUARTER * PACK], BF16, name="z_bf%d" % r, align_bytes=64)
-            src = z_rows[r // 2][:, :, (r % 2) * QUARTER : (r % 2 + 1) * QUARTER].rearrange("p t (c i) -> p c t i", i=4)
-            dst = z_bf[:].rearrange("p (c i t) -> p c t i", i=4, t=PACK)
-            if r < 2:
-                nc.scalar.copy(dst, src)
-            else:
-                nc.vector.tensor_copy(dst, src)
-            z_codes = keep.tile([P, QUARTER], U32, name="z_codes%d" % r, align_bytes=64)
-            z_sc = keep.tile([P, QUARTER], U8, name="z_sc%d" % r, align_bytes=64)
-            nc.vector.quantize_mx(z_codes[:].bitcast(FP8X4), z_sc[:], z_bf[:])
-            y_acc = psum.tile([P, QUARTER], F32, name="y_acc%d" % r, tag="bank%d" % r)
+        chunks = [(0, 0, QUARTER), (1, 0, QUARTER), (3, 0, QUARTER), (2, 0, P), (2, P, QUARTER)]
+        for n, (r, lo, hi) in enumerate(chunks):
+            z_codes = keep.tile([P, hi - lo], U32, name="z_codes%d" % n, align_bytes=64)
+            z_sc = keep.tile([P, hi - lo], U8, name="z_sc%d" % n, align_bytes=64)
+            nc.vector.quantize_mx(z_codes[:].bitcast(FP8X4), z_sc[:], z_bf[r][:, lo:hi, :].rearrange("p c t -> p (c t)"))
+            y_acc = psum.tile([P, hi - lo], F32, name="y_acc%d" % n, tag="bank%d" % (2 + n))
             nc.tensor.matmul_mx(
                 y_acc[:],
                 lhsT=w2_codes[:].bitcast(FP4X4),
@@ -150,15 +155,17 @@ def tile_picked_devox_none_p_kernel(
                 start=True,
                 stop=True,
             )
-            nc.scalar.copy(y[:, r * QUARTER : (r + 1) * QUARTER], y_acc[:])
+            y_cols = y[:, r * QUARTER + lo : r * QUARTER + hi]
+            if n == len(chunks) - 1:
+                nc.vector.tensor_copy(y_cols, y_acc[:])
+            else:
+                nc.scalar.copy(y_cols, y_acc[:])
 
         for a in range(2):
             cols = slice(a * V // 2, (a + 1) * V // 2)
-            part = []
+            prod = [keep.tile([P, V // 2], F32, name="prod%d_%d" % (a, d)) for d in range(2)]
             for d in range(2):
-                prod = keep.tile([P, V // 2], F32, name="prod%d_%d" % (a, d))
-                nc.vector.tensor_tensor(prod[:], y[:].indirect(pos_sb[d][:, 16 * a : 16 * (a + 1)]), gate_sb[d][:, cols], MULT)
-                part.append(prod)
+                nc.vector.tensor_tensor(prod[d][:], y[:].indirect(pos_sb[d][:, 16 * a : 16 * (a + 1)]), gate_sb[d][:, cols], MULT)
             res = keep.tile([P, V // 2], F32, name="res%d" % a)
-            nc.vector.tensor_tensor(res[:], part[0][:], part[1][:], ADD)
+            nc.vector.tensor_tensor(res[:], prod[0][:], prod[1][:], ADD)
             nc.sync.dma_start(out[:, cols], res[:])

@@ -45,25 +45,33 @@ def tile_picked_devox_none_p_kernel(
         for t in range(PACK):
             (nc.vector if t < 2 else nc.gpsimd).memset(up[t][:], 0.0)
 
-        w1_raw = [keep.tile([P, PACK, H], F32, name="w1_raw%d" % g) for g in range(PASSES)]
+        w1_rows = w1.rearrange("(g p j) (hf c) -> hf g p j c", p=P, j=PACK, hf=2)
+        raw = [[None, None], [None, None]]
+
+        def load_w1(hf, g):
+            raw[hf][g] = keep.tile([P, PACK, H // 2], F32, name="raw%d_%d" % (hf, g), tag="raw%d_%d" % (hf, g))
+            nc.sync.dma_start(raw[hf][g][:], w1_rows[hf, g])
+
         xw_all = [keep.tile([P, T], U32, name="xw_all%d" % g) for g in range(PASSES)]
-        w1_rows = w1.rearrange("(g p j) c -> g p j c", p=P, j=PACK)
-        nc.sync.dma_start(w1_raw[0][:], w1_rows[0])
+        x_rows = x_words.rearrange("g p n t -> g p (n t)").bitcast(I32)
+        load_w1(0, 0)
         offs_sb = load_list(offs, "offs_sb")
         for q in range(4):
             nc.sync.dma_start(
                 xs_all[32 * q : 32 * q + 4 * PASSES, :].bitcast(I32),
                 x_scales[:, 4 * q : 4 * q + 4, :].bitcast(I32),
             )
-        nc.sync.dma_start(w1_raw[1][:], w1_rows[1])
-        x_rows = x_words.rearrange("g p n t -> g p (n t)").bitcast(I32)
         nc.sync.dma_start(xw_all[0][:].bitcast(I32), x_rows[0])
-        cell_sb = load_list(cell, "cell_sb")
+        load_w1(0, 1)
         nc.sync.dma_start(xw_all[1][:].bitcast(I32), x_rows[1])
+        cell_sb = load_list(cell, "cell_sb")
+        load_w1(1, 0)
+        load_w1(1, 1)
         emb_sb = [keep.tile([P, U], F32, name="emb_sb%d" % t) for t in range(PACK)]
+        emb_half = emb.rearrange("(hf m t) c -> hf m t c", hf=2, t=PACK)
         emb_rows = emb.rearrange("(p t) c -> t p c", t=PACK)
-        for t in range(PACK):
-            nc.sync.dma_start(emb_sb[t][:], emb_rows[t])
+        for s in range(PACK):
+            nc.sync.dma_start(emb_sb[s][:], emb_half[s, :, 0:2, :] if s < 2 else emb_rows[s])
         w2_codes = keep.tile([P, 2 * N], U8, name="w2_codes", align_bytes=64)
         nc.sync.dma_start(w2_codes[:].bitcast(I32), w2_words[0].bitcast(I32))
         for q in range(4):
@@ -75,17 +83,31 @@ def tile_picked_devox_none_p_kernel(
 
         w1_codes = [keep.tile([P, H], U32, name="w1_codes%d" % g, align_bytes=64) for g in range(PASSES)]
         w1_sc = [keep.tile([P, H], U8, name="w1_sc%d" % g, align_bytes=64) for g in range(PASSES)]
-        for g in range(PASSES):
-            w1_bf = keep.tile([P, H * PACK], BF16, name="w1_bf%d" % g, align_bytes=64)
-            dst = w1_bf[:].rearrange("p (t m j) -> p m t j", t=PACK, j=PACK)
-            src = w1_raw[g][:].rearrange("p j (m t) -> p m t j", t=PACK)
-            nc.vector.tensor_copy(dst[:, : P // 2], src[:, : P // 2])
-            nc.scalar.copy(dst[:, P // 2 :], src[:, P // 2 :])
-            nc.vector.quantize_mx(w1_codes[g][:].bitcast(FP8X4), w1_sc[g][:], w1_bf[:])
+
+        def quantize_w1(g, lo, src):
+            cols = slice(lo, lo + src.shape[1] // PACK)
+            nc.vector.quantize_mx(w1_codes[g][:, cols].bitcast(FP8X4), w1_sc[g][:, cols], src)
+
+        def prepare_w1(hf, g):
+            src = raw[hf][g][:].rearrange("p j (m t) -> p m t j", t=PACK)
+            low = keep.tile([P, H], BF16, name="low%d_%d" % (hf, g), align_bytes=64)
+            high = keep.tile([P, H], BF16, name="high%d_%d" % (hf, g), align_bytes=64)
+            low_dst = low[:].rearrange("p (m e j) -> p m e j", e=2, j=PACK)
+            nc.scalar.copy(high[:].rearrange("p (e m j) -> p m e j", e=2, j=PACK), src[:, :, 2:4, :])
+            if hf == 0:
+                nc.vector.tensor_copy(low_dst, src[:, :, 0:2, :])
+            else:
+                nc.scalar.copy(low_dst, src[:, :, 0:2, :])
+            quantize_w1(g, hf * P, low[:])
+            for e in range(2):
+                quantize_w1(g, (2 + e) * P + hf * P // 2, high[:, e * H // 2 : (e + 1) * H // 2])
+
         xs_pick = keep.tile([P, S], U8, name="xs_pick", align_bytes=64)
         xw_pick = [keep.tile([P, S], U32, name="xw_pick%d" % g, align_bytes=64) for g in range(PASSES)]
+        prepare_w1(0, 0)
         nc.vector.tensor_copy(xs_pick[:], xs_all[:].indirect(offs_sb[:]))
         nc.vector.tensor_copy(xw_pick[0][:], xw_all[0][:].indirect(offs_sb[:]))
+        prepare_w1(0, 1)
         for a in range(2):
             nc.vector.tensor_copy(
                 xw_pick[1][:, a * HALF : (a + 1) * HALF], xw_all[1][:].indirect(offs_sb[:, 16 * a : 16 * (a + 1)])
@@ -93,7 +115,7 @@ def tile_picked_devox_none_p_kernel(
 
         h = [keep.tile([P, S], F32, name="h%d" % t) for t in range(PACK)]
 
-        def first_product(t, lo, hi, bank):
+        def first_product(t, lo, hi, bank, dst):
             acc = psum.tile([P, hi - lo], F32, name="acc%d_%d" % (t, lo), tag="bank%d" % bank)
             cols = slice(t * P, (t + 1) * P)
             for g in range(PASSES):
@@ -106,23 +128,24 @@ def tile_picked_devox_none_p_kernel(
                     start=(g == 0),
                     stop=(g == PASSES - 1),
                 )
-            nc.scalar.activation(h[t][:, lo:hi], acc[:], RELU)
+            nc.scalar.activation(dst, acc[:], RELU)
 
-        def scatter(t, lo, hi):
-            nc.vector.tensor_copy(up[t][:].indirect(cell_sb[:, lo // 16 : hi // 16]), h[t][:, lo:hi])
+        def scatter(t, lo, hi, src):
+            nc.vector.tensor_copy(up[t][:].indirect(cell_sb[:, lo // 16 : hi // 16]), src)
 
-        for t in range(2):
-            first_product(t, 0, P, t)
-            scatter(t, 0, P)
-        for t in range(2):
-            first_product(t, P, HALF, 2 + 2 * t)
-            first_product(t, HALF, S, 3 + 2 * t)
-            scatter(t, P, S)
-        for t in range(2, PACK):
-            first_product(t, 0, S, t - 2)
-            scatter(t, 0, S)
+        for a in range(2):
+            first_product(0, a * P, (a + 1) * P, a, h[0][:, a * P : (a + 1) * P])
+            scatter(0, a * P, (a + 1) * P, h[0][:, a * P : (a + 1) * P])
+        prepare_w1(1, 0)
+        prepare_w1(1, 1)
+        h_last = keep.tile([P, HALF], F32, name="h_last", tag="raw1_1")
+        first_product(0, HALF, S, 2, h_last[:])
+        scatter(0, HALF, S, h_last[:])
+        for t in range(1, PACK):
+            first_product(t, 0, S, 3, h[t][:])
+            scatter(t, 0, S, h[t][:])
 
-        z_pair = [[keep.tile([P, 2, U // 2], BF16, name="z_pair%d_%d" % (u, b)) for b in range(2)] for u in range(2)]
+        planes = [keep.tile([P, 3, U // 2], BF16, name="planes%d" % b) for b in range(2)]
         z_bf = [keep.tile([P, QUARTER, PACK], BF16, name="z_bf%d" % r, align_bytes=64) for r in range(4)]
         for u in range(2):
             for e in range(2):
@@ -130,9 +153,14 @@ def tile_picked_devox_none_p_kernel(
                 eng = nc.vector if t == PACK - 1 else nc.gpsimd
                 for b in range(2):
                     cols = slice(b * U // 2, (b + 1) * U // 2)
-                    eng.tensor_tensor(z_pair[u][b][:, e, :], up[t][:, cols], emb_sb[t][:, cols], ADD)
+                    if u == 0:
+                        z_half = keep.tile([P, U // 2], BF16, name="z_half%d_%d" % (e, b))
+                        eng.tensor_tensor(z_half[:], up[t][:, cols], emb_sb[t][:, cols], ADD)
+                        nc.sync.dma_start(planes[b][64 * e : 64 * (e + 1), 1:3, :], z_half[:])
+                    else:
+                        eng.tensor_tensor(planes[b][:, e, :], up[t][:, cols], emb_sb[t][:, cols], ADD)
             for r in range(4):
-                src = z_pair[u][r // 2][:, :, (r % 2) * QUARTER : (r % 2 + 1) * QUARTER].rearrange("p e c -> p c e")
+                src = planes[r // 2][:, 1 - u : 3 - u, (r % 2) * QUARTER : (r % 2 + 1) * QUARTER].rearrange("p e c -> p c e")
                 dst = z_bf[r][:, :, 2 * u : 2 * u + 2]
                 if u == 1 and r % 2 == 1:
                     nc.vector.tensor_copy(dst, src)

@@ -145,30 +145,30 @@ def tile_picked_devox_none_p_kernel(
             first_product(t, 0, S, 3, h[t][:])
             scatter(t, 0, S, h[t][:])
 
-        planes = [keep.tile([P, 3, U // 2], BF16, name="planes%d" % b) for b in range(2)]
+        planes = [keep.tile([P, PACK, U // 2], BF16, name="planes%d" % b) for b in range(2)]
         z_bf = [keep.tile([P, QUARTER, PACK], BF16, name="z_bf%d" % r, align_bytes=64) for r in range(4)]
-        for u in range(2):
-            for e in range(2):
-                t = 2 * u + e
-                eng = nc.vector if t == PACK - 1 else nc.gpsimd
-                for b in range(2):
-                    cols = slice(b * U // 2, (b + 1) * U // 2)
-                    if u == 0:
-                        z_half = keep.tile([P, U // 2], BF16, name="z_half%d_%d" % (e, b))
-                        eng.tensor_tensor(z_half[:], up[t][:, cols], emb_sb[t][:, cols], ADD)
-                        nc.sync.dma_start(planes[b][64 * e : 64 * (e + 1), 1:3, :], z_half[:])
-                    else:
-                        eng.tensor_tensor(planes[b][:, e, :], up[t][:, cols], emb_sb[t][:, cols], ADD)
-            for r in range(4):
-                src = planes[r // 2][:, 1 - u : 3 - u, (r % 2) * QUARTER : (r % 2 + 1) * QUARTER].rearrange("p e c -> p c e")
-                dst = z_bf[r][:, :, 2 * u : 2 * u + 2]
-                if u == 1 and r % 2 == 1:
-                    nc.vector.tensor_copy(dst, src)
+        for t in range(PACK - 1):
+            for b in range(2):
+                cols = slice(b * U // 2, (b + 1) * U // 2)
+                if t < 2:
+                    z_half = keep.tile([P, U // 2], BF16, name="z_half%d_%d" % (t, b))
+                    nc.gpsimd.tensor_tensor(z_half[:], up[t][:, cols], emb_sb[t][:, cols], ADD)
+                    nc.sync.dma_start(planes[b][64 * t : 64 * (t + 1), 0:2, :], z_half[:])
                 else:
-                    nc.scalar.copy(dst, src)
+                    nc.gpsimd.tensor_tensor(planes[b][:, t, :], up[t][:, cols], emb_sb[t][:, cols], ADD)
+        for lo, hi in ((0, QUARTER), (U // 2, U), (QUARTER, U // 2)):
+            b = lo // (U // 2)
+            nc.vector.tensor_tensor(planes[b][:, 3, lo - b * U // 2 : hi - b * U // 2], up[3][:, lo:hi], emb_sb[3][:, lo:hi], ADD)
+        for r in range(4):
+            src = planes[r // 2][:, :, (r % 2) * QUARTER : (r % 2 + 1) * QUARTER].rearrange("p t (c i) -> p c t i", i=4)
+            dst = z_bf[r][:].rearrange("p (c i) t -> p c t i", i=4)
+            if r < 2:
+                nc.scalar.copy(dst, src)
+            else:
+                nc.vector.tensor_copy(dst, src)
 
         y = keep.tile([P, U], F32, name="y")
-        chunks = [(0, 0, QUARTER), (1, 0, QUARTER), (3, 0, QUARTER), (2, 0, P), (2, P, QUARTER)]
+        chunks = [(0, 0, QUARTER), (2, 0, QUARTER), (3, 0, QUARTER), (1, 0, P), (1, P, QUARTER)]
         for n, (r, lo, hi) in enumerate(chunks):
             z_codes = keep.tile([P, hi - lo], U32, name="z_codes%d" % n, align_bytes=64)
             z_sc = keep.tile([P, hi - lo], U8, name="z_sc%d" % n, align_bytes=64)

@@ -93,11 +93,13 @@ def tile_picked_devox_none_p_kernel(
             low = keep.tile([P, H], BF16, name="low%d_%d" % (hf, g), align_bytes=64)
             high = keep.tile([P, H], BF16, name="high%d_%d" % (hf, g), align_bytes=64)
             low_dst = low[:].rearrange("p (m e j) -> p m e j", e=2, j=PACK)
-            nc.scalar.copy(high[:].rearrange("p (e m j) -> p m e j", e=2, j=PACK), src[:, :, 2:4, :])
+            high_dst = high[:].rearrange("p (e m j) -> p m e j", e=2, j=PACK)
             if hf == 0:
                 nc.vector.tensor_copy(low_dst, src[:, :, 0:2, :])
+                nc.scalar.copy(high_dst, src[:, :, 2:4, :])
             else:
                 nc.scalar.copy(low_dst, src[:, :, 0:2, :])
+                nc.gpsimd.tensor_scalar(high_dst, src[:, :, 2:4, :], 1.0, 0.0, MULT, ADD)
             quantize_w1(g, hf * P, low[:])
             for e in range(2):
                 quantize_w1(g, (2 + e) * P + hf * P // 2, high[:, e * H // 2 : (e + 1) * H // 2])
@@ -141,39 +143,54 @@ def tile_picked_devox_none_p_kernel(
         h_last = keep.tile([P, HALF], F32, name="h_last", tag="raw1_1")
         first_product(0, HALF, S, 2, h_last[:])
         scatter(0, HALF, S, h_last[:])
-        for t in range(1, PACK):
-            first_product(t, 0, S, 3, h[t][:])
+        for a in range(2):
+            first_product(1, a * HALF, (a + 1) * HALF, 3 + a, h[1][:, a * HALF : (a + 1) * HALF])
+        scatter(1, 0, S, h[1][:])
+        for t in range(2, PACK):
+            first_product(t, 0, S, 4, h[t][:])
             scatter(t, 0, S, h[t][:])
 
-        planes = [keep.tile([P, PACK, U // 2], BF16, name="planes%d" % b) for b in range(2)]
-        z_bf = [keep.tile([P, QUARTER, PACK], BF16, name="z_bf%d" % r, align_bytes=64) for r in range(4)]
+        W = U // 2
+        planes = [keep.tile([P, PACK, W], BF16, name="planes%d" % b) for b in range(2)]
         for t in range(PACK - 1):
             for b in range(2):
-                cols = slice(b * U // 2, (b + 1) * U // 2)
+                cols = slice(b * W, (b + 1) * W)
                 if t < 2:
-                    z_half = keep.tile([P, U // 2], BF16, name="z_half%d_%d" % (t, b))
+                    z_half = keep.tile([P, W], BF16, name="z_half%d_%d" % (t, b))
                     nc.gpsimd.tensor_tensor(z_half[:], up[t][:, cols], emb_sb[t][:, cols], ADD)
                     nc.sync.dma_start(planes[b][64 * t : 64 * (t + 1), 0:2, :], z_half[:])
                 else:
                     nc.gpsimd.tensor_tensor(planes[b][:, t, :], up[t][:, cols], emb_sb[t][:, cols], ADD)
-        for lo, hi in ((0, QUARTER), (U // 2, U), (QUARTER, U // 2)):
-            b = lo // (U // 2)
-            nc.vector.tensor_tensor(planes[b][:, 3, lo - b * U // 2 : hi - b * U // 2], up[3][:, lo:hi], emb_sb[3][:, lo:hi], ADD)
-        for r in range(4):
-            src = planes[r // 2][:, :, (r % 2) * QUARTER : (r % 2 + 1) * QUARTER].rearrange("p t (c i) -> p c t i", i=4)
-            dst = z_bf[r][:].rearrange("p (c i) t -> p c t i", i=4)
-            if r < 2:
-                nc.scalar.copy(dst, src)
-            else:
-                nc.vector.tensor_copy(dst, src)
+        for lo, hi in ((0, QUARTER), (W, U), (QUARTER, W)):
+            b = lo // W
+            nc.vector.tensor_tensor(planes[b][:, 3, lo - b * W : hi - b * W], up[3][:, lo:hi], emb_sb[3][:, lo:hi], ADD)
+
+        def interleave(lo, hi, copy):
+            b = lo // W
+            z_bf = keep.tile([P, hi - lo, PACK], BF16, name="z_bf%d" % lo, align_bytes=64)
+            src = planes[b][:, :, lo - b * W : hi - b * W].rearrange("p t (c i) -> p c t i", i=4)
+            copy(z_bf[:].rearrange("p (c i) t -> p c t i", i=4), src)
+            return z_bf
+
+        z_a = interleave(0, 256, nc.scalar.copy)
+        z_b = interleave(256, 512, nc.scalar.copy)
+        z_c = interleave(512, 640, nc.scalar.copy)
+        z_d = interleave(640, U, nc.vector.tensor_copy)
 
         y = keep.tile([P, U], F32, name="y")
-        chunks = [(0, 0, QUARTER), (2, 0, QUARTER), (3, 0, QUARTER), (1, 0, P), (1, P, QUARTER)]
-        for n, (r, lo, hi) in enumerate(chunks):
+        chunks = [
+            (z_a[:], 0, 256, nc.scalar.copy),
+            (z_d[:, :256, :], 640, 896, nc.scalar.copy),
+            (z_d[:, 256:, :], 896, U, nc.vector.tensor_copy),
+            (z_b[:], 256, 512, nc.scalar.copy),
+            (z_c[:], 512, 640, nc.vector.tensor_copy),
+        ]
+        accs = []
+        for n, (z_bf, lo, hi, copy) in enumerate(chunks):
             z_codes = keep.tile([P, hi - lo], U32, name="z_codes%d" % n, align_bytes=64)
             z_sc = keep.tile([P, hi - lo], U8, name="z_sc%d" % n, align_bytes=64)
-            nc.vector.quantize_mx(z_codes[:].bitcast(FP8X4), z_sc[:], z_bf[r][:, lo:hi, :].rearrange("p c t -> p (c t)"))
-            y_acc = psum.tile([P, hi - lo], F32, name="y_acc%d" % n, tag="bank%d" % (2 + n))
+            nc.vector.quantize_mx(z_codes[:].bitcast(FP8X4), z_sc[:], z_bf.rearrange("p c t -> p (c t)"))
+            y_acc = psum.tile([P, hi - lo], F32, name="y_acc%d" % n, tag="bank%d" % ((5 + n) % 8))
             nc.tensor.matmul_mx(
                 y_acc[:],
                 lhsT=w2_codes[:].bitcast(FP4X4),
@@ -183,17 +200,26 @@ def tile_picked_devox_none_p_kernel(
                 start=True,
                 stop=True,
             )
-            y_cols = y[:, r * QUARTER + lo : r * QUARTER + hi]
-            if n == len(chunks) - 1:
-                nc.vector.tensor_copy(y_cols, y_acc[:])
-            else:
-                nc.scalar.copy(y_cols, y_acc[:])
+            accs.append(y_acc)
+        for y_acc, (z_bf, lo, hi, copy) in zip(accs, chunks):
+            copy(y[:, lo:hi], y_acc[:])
 
-        for a in range(2):
-            cols = slice(a * V // 2, (a + 1) * V // 2)
-            prod = [keep.tile([P, V // 2], F32, name="prod%d_%d" % (a, d)) for d in range(2)]
-            for d in range(2):
-                nc.vector.tensor_tensor(prod[d][:], y[:].indirect(pos_sb[d][:, 16 * a : 16 * (a + 1)]), gate_sb[d][:, cols], MULT)
-            res = keep.tile([P, V // 2], F32, name="res%d" % a)
-            nc.vector.tensor_tensor(res[:], prod[0][:], prod[1][:], ADD)
-            nc.sync.dma_start(out[:, cols], res[:])
+        parts = ((0, 384), (384, V))
+        prod = [[keep.tile([P, hi - lo], F32, name="prod%d_%d" % (lo, d)) for d in range(2)] for lo, hi in parts]
+
+        def fetch(a, d):
+            lo, hi = parts[a]
+            nc.vector.tensor_tensor(prod[a][d][:], y[:].indirect(pos_sb[d][:, lo // 16 : hi // 16]), gate_sb[d][:, lo:hi], MULT)
+
+        def finish(a):
+            lo, hi = parts[a]
+            res = keep.tile([P, hi - lo], F32, name="res%d" % a)
+            nc.vector.tensor_tensor(res[:], prod[a][0][:], prod[a][1][:], ADD)
+            nc.sync.dma_start(out[:, lo:hi], res[:])
+
+        fetch(0, 0)
+        fetch(0, 1)
+        fetch(1, 0)
+        finish(0)
+        fetch(1, 1)
+        finish(1)

@@ -135,10 +135,12 @@ def tile_picked_devox_none_p_kernel(
         def scatter(t, lo, hi, src):
             nc.vector.tensor_copy(up[t][:].indirect(cell_sb[:, lo // 16 : hi // 16]), src)
 
-        for a in range(2):
-            first_product(0, a * P, (a + 1) * P, a, h[0][:, a * P : (a + 1) * P])
-            scatter(0, a * P, (a + 1) * P, h[0][:, a * P : (a + 1) * P])
+        first_product(0, 0, P, 0, h[0][:, 0:P])
+        scatter(0, 0, P, h[0][:, 0:P])
         prepare_w1(1, 0)
+        h_mid = keep.tile([P, P], F32, name="h_mid", tag="raw1_0")
+        first_product(0, P, HALF, 1, h_mid[:])
+        scatter(0, P, HALF, h_mid[:])
         prepare_w1(1, 1)
         h_last = keep.tile([P, HALF], F32, name="h_last", tag="raw1_1")
         first_product(0, HALF, S, 2, h_last[:])
@@ -151,31 +153,32 @@ def tile_picked_devox_none_p_kernel(
             scatter(t, 0, S, h[t][:])
 
         W = U // 2
-        planes = [keep.tile([P, PACK, W], BF16, name="planes%d" % b) for b in range(2)]
-        for t in range(PACK - 1):
-            for b in range(2):
-                cols = slice(b * W, (b + 1) * W)
-                if t < 2:
-                    z_half = keep.tile([P, W], BF16, name="z_half%d_%d" % (t, b))
-                    nc.gpsimd.tensor_tensor(z_half[:], up[t][:, cols], emb_sb[t][:, cols], ADD)
-                    nc.sync.dma_start(planes[b][64 * t : 64 * (t + 1), 0:2, :], z_half[:])
-                else:
-                    nc.gpsimd.tensor_tensor(planes[b][:, t, :], up[t][:, cols], emb_sb[t][:, cols], ADD)
-        for lo, hi in ((0, QUARTER), (W, U), (QUARTER, W)):
-            b = lo // W
-            nc.vector.tensor_tensor(planes[b][:, 3, lo - b * W : hi - b * W], up[3][:, lo:hi], emb_sb[3][:, lo:hi], ADD)
+        planes = [keep.tile([P, 3, W], BF16, name="planes%d" % b) for b in range(2)]
+        blocks = [planes[b][:].rearrange("p r (k c) -> p (r k) c", c=QUARTER) for b in range(2)]
+        for t in range(2):
+            width = W if t == 0 else QUARTER
+            for lo in (0, W) if t == 0 else (0, W, QUARTER, W + QUARTER):
+                z_half = keep.tile([P, width], BF16, name="z_half%d_%d" % (t, lo))
+                nc.gpsimd.tensor_tensor(z_half[:], up[t][:, lo : lo + width], emb_sb[t][:, lo : lo + width], ADD)
+                nc.sync.dma_start(planes[lo // W][64 * t : 64 * (t + 1), 1:3, lo % W : lo % W + width], z_half[:])
+        stretches = ((0, 256), (256, 512), (512, 640), (640, U))
+        z_a, z_b, z_c, z_d = [keep.tile([P, hi - lo, PACK], BF16, name="z_bf%d" % lo, align_bytes=64) for lo, hi in stretches]
+        pieces = ((z_a[:], 0, 256), (z_c[:], 512, 640), (z_d[:, :P, :], 640, 768), (z_b[:], 256, 512), (z_d[:, P:, :], 768, U))
 
-        def interleave(lo, hi, copy):
-            b = lo // W
-            z_bf = keep.tile([P, hi - lo, PACK], BF16, name="z_bf%d" % lo, align_bytes=64)
-            src = planes[b][:, :, lo - b * W : hi - b * W].rearrange("p t (c i) -> p c t i", i=4)
-            copy(z_bf[:].rearrange("p (c i) t -> p c t i", i=4), src)
-            return z_bf
-
-        z_a = interleave(0, 256, nc.scalar.copy)
-        z_b = interleave(256, 512, nc.scalar.copy)
-        z_c = interleave(512, 640, nc.scalar.copy)
-        z_d = interleave(640, U, nc.vector.tensor_copy)
+        for z_bf, lo, hi in pieces:
+            src = planes[lo // W][:, 1:3, lo % W : lo % W + hi - lo]
+            nc.scalar.copy(z_bf[:, :, 0:2], src.rearrange("p e c -> p c e"))
+        for b in range(2):
+            cols = slice(b * W, (b + 1) * W)
+            nc.gpsimd.tensor_tensor(planes[b][:, 0, :], up[2][:, cols], emb_sb[2][:, cols], ADD)
+        for r in range(4):
+            cols = slice(r * QUARTER, (r + 1) * QUARTER)
+            nc.vector.tensor_tensor(blocks[r // 2][:, 3 + 2 * (r % 2), :], up[3][:, cols], emb_sb[3][:, cols], ADD)
+        for z_bf, lo, hi in sorted(pieces, key=lambda piece: piece[1]):
+            k = lo // QUARTER % 2
+            src = blocks[lo // W][:, k : 4 + 2 * k : 3 + k, lo % QUARTER : lo % QUARTER + hi - lo]
+            copy = nc.vector.tensor_copy if lo >= 640 else nc.scalar.copy
+            copy(z_bf[:, :, 2:4], src.rearrange("p e c -> p c e"))
 
         y = keep.tile([P, U], F32, name="y")
         chunks = [

@@ -135,12 +135,10 @@ def tile_picked_devox_none_p_kernel(
         def scatter(t, lo, hi, src):
             nc.vector.tensor_copy(up[t][:].indirect(cell_sb[:, lo // 16 : hi // 16]), src)
 
-        first_product(0, 0, P, 0, h[0][:, 0:P])
-        scatter(0, 0, P, h[0][:, 0:P])
+        for a in range(2):
+            first_product(0, a * P, (a + 1) * P, a, h[0][:, a * P : (a + 1) * P])
+            scatter(0, a * P, (a + 1) * P, h[0][:, a * P : (a + 1) * P])
         prepare_w1(1, 0)
-        h_mid = keep.tile([P, P], F32, name="h_mid", tag="raw1_0")
-        first_product(0, P, HALF, 1, h_mid[:])
-        scatter(0, P, HALF, h_mid[:])
         prepare_w1(1, 1)
         h_last = keep.tile([P, HALF], F32, name="h_last", tag="raw1_1")
         first_product(0, HALF, S, 2, h_last[:])

@@ -38,48 +38,34 @@ def tile_picked_devox_none_p_kernel(
             return tile
 
         xs_all = keep.tile([P, T], U8, name="xs_all", align_bytes=64)
-        w2_sc = keep.tile([P, N], U8, name="w2_sc", align_bytes=64)
+        xs_mm = keep.tile([P, PASSES, S], U8, name="xs_mm", align_bytes=64)
         nc.gpsimd.memset(xs_all[:].bitcast(I32), 0)
-        nc.vector.memset(w2_sc[:].bitcast(I32), 0)
+        nc.vector.memset(xs_mm[:].bitcast(I32), 0)
         up = [keep.tile([P, U], F32, name="up%d" % t) for t in range(PACK)]
         for t in range(PACK):
             (nc.vector if t < 2 else nc.gpsimd).memset(up[t][:], 0.0)
 
+        def staged(shape, dtype, name, slot):
+            return keep.tile(shape, dtype, name=name, tag=slot, align_bytes=64)
+
         w1_rows = w1.rearrange("(g p j) (hf c) -> hf g p j c", p=P, j=PACK, hf=2)
         raw = [[None, None], [None, None]]
 
-        def load_w1(hf, g):
-            raw[hf][g] = keep.tile([P, PACK, H // 2], F32, name="raw%d_%d" % (hf, g), tag="raw%d_%d" % (hf, g))
+        def load_w1(hf, g, slot):
+            raw[hf][g] = staged([P, PACK, H // 2], F32, "raw%d_%d" % (hf, g), slot)
             nc.sync.dma_start(raw[hf][g][:], w1_rows[hf, g])
 
         xw_all = [keep.tile([P, T], U32, name="xw_all%d" % g) for g in range(PASSES)]
         x_rows = x_words.rearrange("g p n t -> g p (n t)").bitcast(I32)
-        load_w1(0, 0)
+        load_w1(0, 0, "raw0")
         offs_sb = load_list(offs, "offs_sb")
-        for q in range(4):
-            nc.sync.dma_start(
-                xs_all[32 * q : 32 * q + 4 * PASSES, :].bitcast(I32),
-                x_scales[:, 4 * q : 4 * q + 4, :].bitcast(I32),
-            )
-        nc.sync.dma_start(xw_all[0][:].bitcast(I32), x_rows[0])
-        load_w1(0, 1)
-        nc.sync.dma_start(xw_all[1][:].bitcast(I32), x_rows[1])
+        for g in range(PASSES):
+            nc.sync.dma_start(xs_all[4 * g : P : 8, :].bitcast(I32), x_scales[g].bitcast(I32))
         cell_sb = load_list(cell, "cell_sb")
-        load_w1(1, 0)
-        load_w1(1, 1)
-        emb_sb = [keep.tile([P, U], F32, name="emb_sb%d" % t) for t in range(PACK)]
-        emb_half = emb.rearrange("(hf m t) c -> hf m t c", hf=2, t=PACK)
-        emb_rows = emb.rearrange("(p t) c -> t p c", t=PACK)
-        for s in range(PACK):
-            nc.sync.dma_start(emb_sb[s][:], emb_half[s, :, 0:2, :] if s < 2 else emb_rows[s])
-        w2_codes = keep.tile([P, 2 * N], U8, name="w2_codes", align_bytes=64)
-        nc.sync.dma_start(w2_codes[:].bitcast(I32), w2_words[0].bitcast(I32))
-        for q in range(4):
-            nc.sync.dma_start(w2_sc[32 * q : 32 * q + 4, :].bitcast(I32), w2_scales[0, 4 * q : 4 * q + 4, :].bitcast(I32))
         pos_sb = [load_list(pos1, "pos1_sb"), load_list(pos2, "pos2_sb")]
-        gate_sb = [keep.tile([P, V], F32, name="gate_sb%d" % d) for d in range(2)]
-        for d in range(2):
-            nc.sync.dma_start(gate_sb[d][:], gate[d])
+        nc.sync.dma_start(xw_all[0][:].bitcast(I32), x_rows[0])
+        load_w1(0, 1, "raw1")
+        nc.sync.dma_start(xw_all[1][:].bitcast(I32), x_rows[1])
 
         w1_codes = [keep.tile([P, H], U32, name="w1_codes%d" % g, align_bytes=64) for g in range(PASSES)]
         w1_sc = [keep.tile([P, H], U8, name="w1_sc%d" % g, align_bytes=64) for g in range(PASSES)]
@@ -88,10 +74,10 @@ def tile_picked_devox_none_p_kernel(
             cols = slice(lo, lo + src.shape[1] // PACK)
             nc.vector.quantize_mx(w1_codes[g][:, cols].bitcast(FP8X4), w1_sc[g][:, cols], src)
 
-        def prepare_w1(hf, g):
+        def round_w1(hf, g):
             src = raw[hf][g][:].rearrange("p j (m t) -> p m t j", t=PACK)
-            low = keep.tile([P, H], BF16, name="low%d_%d" % (hf, g), align_bytes=64)
-            high = keep.tile([P, H], BF16, name="high%d_%d" % (hf, g), align_bytes=64)
+            low = staged([P, H], BF16, "low%d_%d" % (hf, g), "low%d_%d" % (hf, g))
+            high = staged([P, H], BF16, "high%d_%d" % (hf, g), "high%d_%d" % (hf, g))
             low_dst = low[:].rearrange("p (m e j) -> p m e j", e=2, j=PACK)
             high_dst = high[:].rearrange("p (e m j) -> p m e j", e=2, j=PACK)
             if hf == 0:
@@ -100,16 +86,38 @@ def tile_picked_devox_none_p_kernel(
             else:
                 nc.scalar.copy(low_dst, src[:, :, 0:2, :])
                 nc.gpsimd.tensor_scalar(high_dst, src[:, :, 2:4, :], 1.0, 0.0, MULT, ADD)
+            return low, high
+
+        def pack_w1(hf, g, low, high):
             quantize_w1(g, hf * P, low[:])
             for e in range(2):
                 quantize_w1(g, (2 + e) * P + hf * P // 2, high[:, e * H // 2 : (e + 1) * H // 2])
 
+        def prepare_w1(hf, g):
+            pack_w1(hf, g, *round_w1(hf, g))
+
         xs_pick = keep.tile([P, S], U8, name="xs_pick", align_bytes=64)
         xw_pick = [keep.tile([P, S], U32, name="xw_pick%d" % g, align_bytes=64) for g in range(PASSES)]
-        prepare_w1(0, 0)
+        rounded = round_w1(0, 0)
         nc.vector.tensor_copy(xs_pick[:], xs_all[:].indirect(offs_sb[:]))
+        for q in range(4):
+            nc.sync.dma_start(xs_mm[32 * q : 32 * q + 4].bitcast(I32), xs_pick[32 * q : 32 * q + 32 : 4, :].bitcast(I32))
+        pack_w1(0, 0, *rounded)
+        load_w1(1, 0, "low0_0")
+        load_w1(1, 1, "high0_0")
         nc.vector.tensor_copy(xw_pick[0][:], xw_all[0][:].indirect(offs_sb[:]))
         prepare_w1(0, 1)
+        emb_half = emb.rearrange("(hf m t) c -> hf m t c", hf=2, t=PACK)
+        emb_rows = emb.rearrange("(p t) c -> t p c", t=PACK)
+        emb_sb = []
+
+        def load_emb(slot):
+            s = len(emb_sb)
+            emb_sb.append(staged([P, U], F32, "emb_sb%d" % s, slot))
+            nc.sync.dma_start(emb_sb[s][:], emb_half[s, :, 0:2, :] if s < 2 else emb_rows[s])
+
+        load_emb("low0_1")
+        load_emb("high0_1")
         for a in range(2):
             nc.vector.tensor_copy(
                 xw_pick[1][:, a * HALF : (a + 1) * HALF], xw_all[1][:].indirect(offs_sb[:, 16 * a : 16 * (a + 1)])
@@ -126,7 +134,7 @@ def tile_picked_devox_none_p_kernel(
                     lhsT=w1_codes[g][:, cols].bitcast(FP8X4),
                     lhsT_scale=w1_sc[g][:, cols],
                     rhs=xw_pick[g][:, lo:hi].bitcast(FP8X4),
-                    rhs_scale=xs_pick[4 * g :, lo:hi],
+                    rhs_scale=xs_mm[:, g, lo:hi],
                     start=(g == 0),
                     stop=(g == PASSES - 1),
                 )
@@ -140,9 +148,21 @@ def tile_picked_devox_none_p_kernel(
             scatter(0, a * P, (a + 1) * P, h[0][:, a * P : (a + 1) * P])
         prepare_w1(1, 0)
         prepare_w1(1, 1)
-        h_last = keep.tile([P, HALF], F32, name="h_last", tag="raw1_1")
+        h_last = staged([P, HALF], F32, "h_last", "high0_0")
+        load_emb("low0_0")
+        load_emb("low1_0")
+        w2_codes = staged([P, 2 * N], U8, "w2_codes", "low1_1")
+        nc.sync.dma_start(w2_codes[:].bitcast(I32), w2_words[0].bitcast(I32))
+        gate_sb = []
+        for d in range(2):
+            gate_sb.append(staged([P, V], F32, "gate_sb%d" % d, "high1_%d" % d))
+            nc.sync.dma_start(gate_sb[d][:], gate[d])
         first_product(0, HALF, S, 2, h_last[:])
         scatter(0, HALF, S, h_last[:])
+        w2_sc = staged([P, N], U8, "w2_sc", "high0_0")
+        nc.gpsimd.memset(w2_sc[:].bitcast(I32), 0)
+        for q in range(4):
+            nc.sync.dma_start(w2_sc[32 * q : 32 * q + 4, :].bitcast(I32), w2_scales[0, 4 * q : 4 * q + 4, :].bitcast(I32))
         for a in range(2):
             first_product(1, a * HALF, (a + 1) * HALF, 3 + a, h[1][:, a * HALF : (a + 1) * HALF])
         scatter(1, 0, S, h[1][:])

@@ -59,13 +59,13 @@ def tile_picked_devox_none_p_kernel(
         x_rows = x_words.rearrange("g p n t -> g p (n t)").bitcast(I32)
         load_w1(0, 0, "raw0")
         offs_sb = load_list(offs, "offs_sb")
-        for g in range(PASSES):
-            nc.sync.dma_start(xs_all[4 * g : P : 8, :].bitcast(I32), x_scales[g].bitcast(I32))
+        nc.sync.dma_start(xs_all[0:P:4, :].bitcast(I32), x_scales.bitcast(I32).rearrange("g i c -> i g c"))
         cell_sb = load_list(cell, "cell_sb")
-        pos_sb = [load_list(pos1, "pos1_sb"), load_list(pos2, "pos2_sb")]
+        pos_sb = [load_list(pos1, "pos1_sb")]
         nc.sync.dma_start(xw_all[0][:].bitcast(I32), x_rows[0])
         load_w1(0, 1, "raw1")
         nc.sync.dma_start(xw_all[1][:].bitcast(I32), x_rows[1])
+        pos_sb.append(load_list(pos2, "pos2_sb"))
 
         w1_codes = [keep.tile([P, H], U32, name="w1_codes%d" % g, align_bytes=64) for g in range(PASSES)]
         w1_sc = [keep.tile([P, H], U8, name="w1_sc%d" % g, align_bytes=64) for g in range(PASSES)]

@@ -143,9 +143,8 @@ def tile_picked_devox_none_p_kernel(
         def scatter(t, lo, hi, src):
             nc.vector.tensor_copy(up[t][:].indirect(cell_sb[:, lo // 16 : hi // 16]), src)
 
-        for a in range(2):
-            first_product(0, a * P, (a + 1) * P, a, h[0][:, a * P : (a + 1) * P])
-            scatter(0, a * P, (a + 1) * P, h[0][:, a * P : (a + 1) * P])
+        first_product(0, 0, HALF, 0, h[0][:, 0:HALF])
+        scatter(0, 0, HALF, h[0][:, 0:HALF])
         prepare_w1(1, 0)
         prepare_w1(1, 1)
         h_last = staged([P, HALF], F32, "h_last", "high0_0")

@@ -178,32 +178,40 @@ def tile_picked_devox_none_p_kernel(
                 z_half = keep.tile([P, width], BF16, name="z_half%d_%d" % (t, lo))
                 nc.gpsimd.tensor_tensor(z_half[:], up[t][:, lo : lo + width], emb_sb[t][:, lo : lo + width], ADD)
                 nc.sync.dma_start(planes[lo // W][64 * t : 64 * (t + 1), 1:3, lo % W : lo % W + width], z_half[:])
-        stretches = ((0, 256), (256, 512), (512, 640), (640, U))
+        stretches = ((0, 256), (256, 512), (512, 768), (768, U))
         z_a, z_b, z_c, z_d = [keep.tile([P, hi - lo, PACK], BF16, name="z_bf%d" % lo, align_bytes=64) for lo, hi in stretches]
-        pieces = ((z_a[:], 0, 256), (z_c[:], 512, 640), (z_d[:, :P, :], 640, 768), (z_b[:], 256, 512), (z_d[:, P:, :], 768, U))
+        early = ((z_a[:], 0, 256), (z_c[:], 512, 768), (z_b[:], 256, 512), (z_d[:], 768, U))
+        pieces = (
+            (z_a[:, :P, :], 0, P),
+            (z_a[:, P:, :], P, 256),
+            (z_b[:], 256, 512),
+            (z_c[:, :P, :], 512, 640),
+            (z_c[:, P:, :], 640, 768),
+            (z_d[:], 768, U),
+        )
 
-        for z_bf, lo, hi in pieces:
+        for z_bf, lo, hi in early:
             src = planes[lo // W][:, 1:3, lo % W : lo % W + hi - lo]
             nc.scalar.copy(z_bf[:, :, 0:2], src.rearrange("p e c -> p c e"))
         for b in range(2):
             cols = slice(b * W, (b + 1) * W)
             nc.gpsimd.tensor_tensor(planes[b][:, 0, :], up[2][:, cols], emb_sb[2][:, cols], ADD)
-        for r in range(4):
-            cols = slice(r * QUARTER, (r + 1) * QUARTER)
-            nc.vector.tensor_tensor(blocks[r // 2][:, 3 + 2 * (r % 2), :], up[3][:, cols], emb_sb[3][:, cols], ADD)
-        for z_bf, lo, hi in sorted(pieces, key=lambda piece: piece[1]):
+        for lo, hi in ((0, P), (P, 256), (256, 512), (768, U), (512, 768)):
+            dst = blocks[lo // W][:, 3 + 2 * (lo // QUARTER % 2), lo % QUARTER : lo % QUARTER + hi - lo]
+            nc.vector.tensor_tensor(dst, up[3][:, lo:hi], emb_sb[3][:, lo:hi], ADD)
+        for z_bf, lo, hi in pieces:
             k = lo // QUARTER % 2
             src = blocks[lo // W][:, k : 4 + 2 * k : 3 + k, lo % QUARTER : lo % QUARTER + hi - lo]
-            copy = nc.vector.tensor_copy if lo >= 640 else nc.scalar.copy
+            copy = nc.vector.tensor_copy if lo >= 768 else nc.scalar.copy
             copy(z_bf[:, :, 2:4], src.rearrange("p e c -> p c e"))
 
         y = keep.tile([P, U], F32, name="y")
         chunks = [
-            (z_a[:], 0, 256, nc.scalar.copy),
-            (z_d[:, :256, :], 640, 896, nc.scalar.copy),
-            (z_d[:, 256:, :], 896, U, nc.vector.tensor_copy),
+            (z_a[:], 0, 256, nc.vector.tensor_copy),
+            (z_d[:], 768, U, nc.vector.tensor_copy),
             (z_b[:], 256, 512, nc.scalar.copy),
-            (z_c[:], 512, 640, nc.vector.tensor_copy),
+            (z_c[:, :P, :], 512, 640, nc.scalar.copy),
+            (z_c[:, P:, :], 640, 768, nc.vector.tensor_copy),
         ]
         accs = []
         for n, (z_bf, lo, hi, copy) in enumerate(chunks):
@@ -231,15 +239,16 @@ def tile_picked_devox_none_p_kernel(
             lo, hi = parts[a]
             nc.vector.tensor_tensor(prod[a][d][:], y[:].indirect(pos_sb[d][:, lo // 16 : hi // 16]), gate_sb[d][:, lo:hi], MULT)
 
-        def finish(a):
-            lo, hi = parts[a]
-            res = keep.tile([P, hi - lo], F32, name="res%d" % a)
-            nc.vector.tensor_tensor(res[:], prod[a][0][:], prod[a][1][:], ADD)
+        def finish(a, lo, hi):
+            cols = slice(lo - parts[a][0], hi - parts[a][0])
+            res = keep.tile([P, hi - lo], F32, name="res%d" % lo)
+            nc.vector.tensor_tensor(res[:], prod[a][0][:, cols], prod[a][1][:, cols], ADD)
             nc.sync.dma_start(out[:, lo:hi], res[:])
 
         fetch(0, 0)
         fetch(0, 1)
         fetch(1, 0)
-        finish(0)
+        finish(0, 0, 256)
         fetch(1, 1)
-        finish(1)
+        finish(0, 256, 384)
+        finish(1, 384, V)

@@ -182,12 +182,13 @@ def tile_picked_devox_none_p_kernel(
         z_a, z_b, z_c, z_d = [keep.tile([P, hi - lo, PACK], BF16, name="z_bf%d" % lo, align_bytes=64) for lo, hi in stretches]
         early = ((z_a[:], 0, 256), (z_c[:], 512, 768), (z_b[:], 256, 512), (z_d[:], 768, U))
         pieces = (
-            (z_a[:, :P, :], 0, P),
-            (z_a[:, P:, :], P, 256),
+            (z_a[:, :64, :], 0, 64),
+            (z_a[:, 64:, :], 64, 256),
             (z_b[:], 256, 512),
             (z_c[:, :P, :], 512, 640),
-            (z_c[:, P:, :], 640, 768),
+            (z_c[:, P:192, :], 640, 704),
             (z_d[:], 768, U),
+            (z_c[:, 192:, :], 704, 768),
         )
 
         for z_bf, lo, hi in early:
@@ -196,22 +197,22 @@ def tile_picked_devox_none_p_kernel(
         for b in range(2):
             cols = slice(b * W, (b + 1) * W)
             nc.gpsimd.tensor_tensor(planes[b][:, 0, :], up[2][:, cols], emb_sb[2][:, cols], ADD)
-        for lo, hi in ((0, P), (P, 256), (256, 512), (768, U), (512, 768)):
+        for lo, hi in ((0, 64), (64, 256), (256, 512), (768, U), (512, 768)):
             dst = blocks[lo // W][:, 3 + 2 * (lo // QUARTER % 2), lo % QUARTER : lo % QUARTER + hi - lo]
             nc.vector.tensor_tensor(dst, up[3][:, lo:hi], emb_sb[3][:, lo:hi], ADD)
         for z_bf, lo, hi in pieces:
             k = lo // QUARTER % 2
             src = blocks[lo // W][:, k : 4 + 2 * k : 3 + k, lo % QUARTER : lo % QUARTER + hi - lo]
-            copy = nc.vector.tensor_copy if lo >= 768 else nc.scalar.copy
+            copy = nc.vector.tensor_copy if lo >= 704 else nc.scalar.copy
             copy(z_bf[:, :, 2:4], src.rearrange("p e c -> p c e"))
 
         y = keep.tile([P, U], F32, name="y")
         chunks = [
-            (z_a[:], 0, 256, nc.vector.tensor_copy),
+            (z_a[:], 0, 256, nc.scalar.copy),
             (z_d[:], 768, U, nc.vector.tensor_copy),
             (z_b[:], 256, 512, nc.scalar.copy),
-            (z_c[:, :P, :], 512, 640, nc.scalar.copy),
-            (z_c[:, P:, :], 640, 768, nc.vector.tensor_copy),
+            (z_c[:, :P, :], 512, 640, nc.vector.tensor_copy),
+            (z_c[:, P:, :], 640, 768, nc.scalar.copy),
         ]
         accs = []
         for n, (z_bf, lo, hi, copy) in enumerate(chunks):

@@ -186,9 +186,9 @@ def tile_picked_devox_none_p_kernel(
             (z_a[:, 64:, :], 64, 256),
             (z_b[:], 256, 512),
             (z_c[:, :P, :], 512, 640),
-            (z_c[:, P:192, :], 640, 704),
+            (z_c[:, P:160, :], 640, 672),
             (z_d[:], 768, U),
-            (z_c[:, 192:, :], 704, 768),
+            (z_c[:, 160:, :], 672, 768),
         )
 
         for z_bf, lo, hi in early:
@@ -203,7 +203,7 @@ def tile_picked_devox_none_p_kernel(
         for z_bf, lo, hi in pieces:
             k = lo // QUARTER % 2
             src = blocks[lo // W][:, k : 4 + 2 * k : 3 + k, lo % QUARTER : lo % QUARTER + hi - lo]
-            copy = nc.vector.tensor_copy if lo >= 704 else nc.scalar.copy
+            copy = nc.vector.tensor_copy if lo >= 672 else nc.scalar.copy
             copy(z_bf[:, :, 2:4], src.rearrange("p e c -> p c e"))
 
         y = keep.tile([P, U], F32, name="y")
@@ -244,7 +244,7 @@ def tile_picked_devox_none_p_kernel(
             cols = slice(lo - parts[a][0], hi - parts[a][0])
             res = keep.tile([P, hi - lo], F32, name="res%d" % lo)
             nc.vector.tensor_tensor(res[:], prod[a][0][:, cols], prod[a][1][:, cols], ADD)
-            nc.sync.dma_start(out[:, lo:hi], res[:])
+            (nc.scalar if hi == V else nc.sync).dma_start(out[:, lo:hi], res[:])
 
         fetch(0, 0)
         fetch(0, 1)

@@ -1,6 +1,7 @@
 from contextlib import ExitStack
 
 import concourse.mybir as mybir
+from concourse.masks import make_identity
 
 K, T, S, V, H, N, U = 1024, 2048, 512, 512, 512, 128, 1024
 FLOPS = 2 * K * H * S + 2 * H * N * U
@@ -109,15 +110,14 @@ def tile_picked_devox_none_p_kernel(
         prepare_w1(0, 1)
         emb_half = emb.rearrange("(hf m t) c -> hf m t c", hf=2, t=PACK)
         emb_rows = emb.rearrange("(p t) c -> t p c", t=PACK)
-        emb_sb = []
+        emb_sb = [None] * PACK
 
-        def load_emb(slot):
-            s = len(emb_sb)
-            emb_sb.append(staged([P, U], F32, "emb_sb%d" % s, slot))
+        def load_emb(s, slot):
+            emb_sb[s] = staged([P, U], F32, "emb_sb%d" % s, slot)
             nc.sync.dma_start(emb_sb[s][:], emb_half[s, :, 0:2, :] if s < 2 else emb_rows[s])
 
-        load_emb("low0_1")
-        load_emb("high0_1")
+        load_emb(0, "low0_1")
+        load_emb(1, "high0_1")
         for a in range(2):
             nc.vector.tensor_copy(
                 xw_pick[1][:, a * HALF : (a + 1) * HALF], xw_all[1][:].indirect(offs_sb[:, 16 * a : 16 * (a + 1)])
@@ -148,8 +148,8 @@ def tile_picked_devox_none_p_kernel(
         prepare_w1(1, 0)
         prepare_w1(1, 1)
         h_last = staged([P, HALF], F32, "h_last", "high0_0")
-        load_emb("low0_0")
-        load_emb("low1_0")
+        load_emb(3, "low0_0")
+        load_emb(2, "low1_0")
         w2_codes = staged([P, 2 * N], U8, "w2_codes", "low1_1")
         nc.sync.dma_start(w2_codes[:].bitcast(I32), w2_words[0].bitcast(I32))
         gate_sb = []
@@ -170,6 +170,19 @@ def tile_picked_devox_none_p_kernel(
             scatter(t, 0, S, h[t][:])
 
         W = U // 2
+        ident = keep.tile([P, P], F32, name="ident")
+        make_identity(nc, ident[:])
+        emb_ps = []
+        for b, width in enumerate((W, QUARTER)):
+            turned = psum.tile([P, width], F32, name="turned%d" % b, tag="bank%d" % (5 + b))
+            for c in range(0, width, P):
+                nc.tensor.transpose(turned[:, c : c + P], emb_sb[3][:, b * W + c : b * W + c + P], ident[:])
+            turned_sb = keep.tile([P, width], F32, name="turned_sb%d" % b)
+            nc.scalar.copy(turned_sb[:], turned[:])
+            back = psum.tile([P, width], F32, name="emb_ps%d" % b, tag="bank%d" % (2 + b))
+            for c in range(0, width, P):
+                nc.tensor.transpose(back[:, c : c + P], turned_sb[:, c : c + P], ident[:])
+            emb_ps.append(back)
         planes = [keep.tile([P, 3, W], BF16, name="planes%d" % b) for b in range(2)]
         blocks = [planes[b][:].rearrange("p r (k c) -> p (r k) c", c=QUARTER) for b in range(2)]
         for t in range(2):
@@ -185,34 +198,32 @@ def tile_picked_devox_none_p_kernel(
             (z_a[:, :64, :], 0, 64),
             (z_a[:, 64:, :], 64, 256),
             (z_b[:], 256, 512),
-            (z_c[:, :P, :], 512, 640),
-            (z_c[:, P:160, :], 640, 672),
-            (z_d[:], 768, U),
-            (z_c[:, 160:, :], 672, 768),
+            (z_c[:], 512, 768),
         )
 
+        nc.gpsimd.tensor_tensor(z_d[:, :, 2], up[2][:, 768:U], emb_sb[2][:, 768:U], ADD)
         for z_bf, lo, hi in early:
             src = planes[lo // W][:, 1:3, lo % W : lo % W + hi - lo]
             nc.scalar.copy(z_bf[:, :, 0:2], src.rearrange("p e c -> p c e"))
-        for b in range(2):
-            cols = slice(b * W, (b + 1) * W)
-            nc.gpsimd.tensor_tensor(planes[b][:, 0, :], up[2][:, cols], emb_sb[2][:, cols], ADD)
-        for lo, hi in ((0, 64), (64, 256), (256, 512), (768, U), (512, 768)):
+        for lo, hi in ((0, W), (W, 768)):
+            nc.gpsimd.tensor_tensor(planes[lo // W][:, 0, 0 : hi - lo], up[2][:, lo:hi], emb_sb[2][:, lo:hi], ADD)
+        nc.gpsimd.tensor_tensor(z_d[:, :, 3], up[3][:, 768:U], emb_sb[3][:, 768:U], ADD)
+        for lo, hi in ((0, 64), (64, 256), (256, 512), (512, 768)):
             dst = blocks[lo // W][:, 3 + 2 * (lo // QUARTER % 2), lo % QUARTER : lo % QUARTER + hi - lo]
-            nc.vector.tensor_tensor(dst, up[3][:, lo:hi], emb_sb[3][:, lo:hi], ADD)
+            nc.vector.tensor_tensor(dst, up[3][:, lo:hi], emb_ps[lo // W][:, lo % W : lo % W + hi - lo], ADD)
         for z_bf, lo, hi in pieces:
             k = lo // QUARTER % 2
             src = blocks[lo // W][:, k : 4 + 2 * k : 3 + k, lo % QUARTER : lo % QUARTER + hi - lo]
-            copy = nc.vector.tensor_copy if lo >= 672 else nc.scalar.copy
+            copy = nc.vector.tensor_copy if lo >= W else nc.scalar.copy
             copy(z_bf[:, :, 2:4], src.rearrange("p e c -> p c e"))
 
         y = keep.tile([P, U], F32, name="y")
         chunks = [
+            (z_d[:], 768, U, nc.scalar.copy),
             (z_a[:], 0, 256, nc.scalar.copy),
-            (z_d[:], 768, U, nc.vector.tensor_copy),
-            (z_b[:], 256, 512, nc.scalar.copy),
-            (z_c[:, :P, :], 512, 640, nc.vector.tensor_copy),
-            (z_c[:, P:, :], 640, 768, nc.scalar.copy),
+            (z_c[:], 512, 768, nc.vector.tensor_copy),
+            (z_b[:, :P, :], 256, 384, nc.scalar.copy),
+            (z_b[:, P:, :], 384, 512, nc.vector.tensor_copy),
         ]
         accs = []
         for n, (z_bf, lo, hi, copy) in enumerate(chunks):

@@ -43,6 +43,8 @@ def tile_picked_devox_none_p_kernel(
         nc.gpsimd.memset(xs_all[:].bitcast(I32), 0)
         nc.vector.memset(xs_mm[:].bitcast(I32), 0)
         up = [keep.tile([P, U], F32, name="up%d" % t) for t in range(PACK)]
+        up_first = keep.tile([P, U], F32, name="up_first")
+        nc.vector.memset(up_first[:], 0.0)
         for t in range(PACK):
             (nc.vector if t < 2 else nc.gpsimd).memset(up[t][:], 0.0)
 
@@ -143,8 +145,10 @@ def tile_picked_devox_none_p_kernel(
         def scatter(t, lo, hi, src):
             nc.vector.tensor_copy(up[t][:].indirect(cell_sb[:, lo // 16 : hi // 16]), src)
 
-        first_product(0, 0, HALF, 0, h[0][:, 0:HALF])
-        scatter(0, 0, HALF, h[0][:, 0:HALF])
+        first_product(0, 0, P, 0, h[0][:, 0:P])
+        first_product(0, P, HALF, 1, h[0][:, P:HALF])
+        nc.vector.tensor_copy(up_first[:].indirect(cell_sb[:, 0 : P // 16]), h[0][:, 0:P])
+        scatter(0, P, HALF, h[0][:, P:HALF])
         prepare_w1(1, 0)
         prepare_w1(1, 1)
         h_last = staged([P, HALF], F32, "h_last", "high0_0")
@@ -154,8 +158,12 @@ def tile_picked_devox_none_p_kernel(
         nc.sync.dma_start(w2_codes[:].bitcast(I32), w2_words[0].bitcast(I32))
         gate_sb = []
         for d in range(2):
-            gate_sb.append(staged([P, V], F32, "gate_sb%d" % d, "high1_%d" % d))
+            gate_sb.append(staged([P, V], F32, "gate_sb%d" % d, "high1_0" if d == 0 else "raw1"))
             nc.sync.dma_start(gate_sb[d][:], gate[d])
+        emb_first = staged([P, U], F32, "emb_first", "high1_1")
+        for lo in (0, U // 2):
+            cols = slice(lo, lo + U // 2)
+            nc.gpsimd.tensor_tensor(emb_first[:, cols], up_first[:, cols], emb_sb[0][:, cols], ADD)
         first_product(0, HALF, S, 2, h_last[:])
         scatter(0, HALF, S, h_last[:])
         w2_sc = staged([P, N], U8, "w2_sc", "high0_0")
@@ -189,7 +197,7 @@ def tile_picked_devox_none_p_kernel(
             width = W if t == 0 else QUARTER
             for lo in (0, W) if t == 0 else (0, W, QUARTER, W + QUARTER):
                 z_half = keep.tile([P, width], BF16, name="z_half%d_%d" % (t, lo))
-                nc.gpsimd.tensor_tensor(z_half[:], up[t][:, lo : lo + width], emb_sb[t][:, lo : lo + width], ADD)
+                nc.gpsimd.tensor_tensor(z_half[:], up[t][:, lo : lo + width], (emb_first if t == 0 else emb_sb[t])[:, lo : lo + width], ADD)
                 nc.sync.dma_start(planes[lo // W][64 * t : 64 * (t + 1), 1:3, lo % W : lo % W + width], z_half[:])
         stretches = ((0, 256), (256, 512), (512, 768), (768, U))
         z_a, z_b, z_c, z_d = [keep.tile([P, hi - lo, PACK], BF16, name="z_bf%d" % lo, align_bytes=64) for lo, hi in stretches]
@@ -197,7 +205,8 @@ def tile_picked_devox_none_p_kernel(
         pieces = (
             (z_a[:, :64, :], 0, 64),
             (z_a[:, 64:, :], 64, 256),
-            (z_b[:], 256, 512),
+            (z_b[:, :P, :], 256, 384),
+            (z_b[:, P:, :], 384, 512),
             (z_c[:], 512, 768),
         )
 
@@ -222,8 +231,8 @@ def tile_picked_devox_none_p_kernel(
             (z_d[:], 768, U, nc.scalar.copy),
             (z_a[:], 0, 256, nc.scalar.copy),
             (z_c[:], 512, 768, nc.vector.tensor_copy),
-            (z_b[:, :P, :], 256, 384, nc.scalar.copy),
-            (z_b[:, P:, :], 384, 512, nc.vector.tensor_copy),
+            (z_b[:, :P, :], 256, 384, nc.vector.tensor_copy),
+            (z_b[:, P:, :], 384, 512, nc.scalar.copy),
         ]
         accs = []
         for n, (z_bf, lo, hi, copy) in enumerate(chunks):

@@ -103,7 +103,7 @@ def tile_picked_devox_none_p_kernel(
         xw_pick = [keep.tile([P, S], U32, name="xw_pick%d" % g, align_bytes=64) for g in range(PASSES)]
         rounded = round_w1(0, 0)
         nc.vector.tensor_copy(xs_pick[:], xs_all[:].indirect(offs_sb[:]))
-        for q in range(4):
+        for q in (0, 2, 1, 3):
             nc.sync.dma_start(xs_mm[32 * q : 32 * q + 4].bitcast(I32), xs_pick[32 * q : 32 * q + 32 : 4, :].bitcast(I32))
         pack_w1(0, 0, *rounded)
         load_w1(1, 0, "low0_0")

@@ -31,6 +31,7 @@ def tile_picked_devox_none_p_kernel(
     nc = tc.nc
     with ExitStack() as ctx:
         keep = ctx.enter_context(tc.tile_pool(name="keep", bufs=1))
+        laid = ctx.enter_context(tc.tile_pool(name="laid", bufs=1))
         psum = ctx.enter_context(tc.psum_pool(name="psum", bufs=1))
 
         def load_list(src, name):
@@ -42,7 +43,8 @@ def tile_picked_devox_none_p_kernel(
         xs_mm = keep.tile([P, PASSES, S], U8, name="xs_mm", align_bytes=64)
         nc.gpsimd.memset(xs_all[:].bitcast(I32), 0)
         nc.vector.memset(xs_mm[:].bitcast(I32), 0)
-        up = [keep.tile([P, U], F32, name="up%d" % t) for t in range(PACK)]
+        up = [keep.tile([P, U], F32, name="up%d" % t) for t in range(PACK - 1)]
+        up.append(laid.tile([P, U], F32, name="up3", offset=8192, align_bytes=64))
         up_first = keep.tile([P, U], F32, name="up_first")
         nc.vector.memset(up_first[:], 0.0)
         for t in range(PACK):
@@ -50,6 +52,9 @@ def tile_picked_devox_none_p_kernel(
 
         def staged(shape, dtype, name, slot):
             return keep.tile(shape, dtype, name=name, tag=slot, align_bytes=64)
+
+        def placed(shape, dtype, name, offset):
+            return laid.tile(shape, dtype, name=name, offset=offset, align_bytes=64)
 
         w1_rows = w1.rearrange("(g p j) (hf c) -> hf g p j c", p=P, j=PACK, hf=2)
         raw = [[None, None], [None, None]]
@@ -152,18 +157,14 @@ def tile_picked_devox_none_p_kernel(
         prepare_w1(1, 0)
         prepare_w1(1, 1)
         h_last = staged([P, HALF], F32, "h_last", "high0_0")
-        load_emb(3, "low0_0")
-        load_emb(2, "low1_0")
+        load_emb(2, "low0_0")
+        load_emb(3, "low1_0")
         w2_codes = staged([P, 2 * N], U8, "w2_codes", "low1_1")
         nc.sync.dma_start(w2_codes[:].bitcast(I32), w2_words[0].bitcast(I32))
         gate_sb = []
         for d in range(2):
             gate_sb.append(staged([P, V], F32, "gate_sb%d" % d, "high1_0" if d == 0 else "raw1"))
             nc.sync.dma_start(gate_sb[d][:], gate[d])
-        emb_first = staged([P, U], F32, "emb_first", "high1_1")
-        for lo in (0, U // 2):
-            cols = slice(lo, lo + U // 2)
-            nc.gpsimd.tensor_tensor(emb_first[:, cols], up_first[:, cols], emb_sb[0][:, cols], ADD)
         first_product(0, HALF, S, 2, h_last[:])
         scatter(0, HALF, S, h_last[:])
         w2_sc = staged([P, N], U8, "w2_sc", "high0_0")
@@ -174,57 +175,83 @@ def tile_picked_devox_none_p_kernel(
             first_product(1, a * HALF, (a + 1) * HALF, 3 + a, h[1][:, a * HALF : (a + 1) * HALF])
         scatter(1, 0, S, h[1][:])
         for t in range(2, PACK):
-            first_product(t, 0, S, 4, h[t][:])
+            first_product(t, 0, S, 1 + t, h[t][:])
             scatter(t, 0, S, h[t][:])
 
-        W = U // 2
-        ident = keep.tile([P, P], F32, name="ident")
+        ident = staged([P, P], F32, "ident", "high1_1")
         make_identity(nc, ident[:])
-        emb_ps = []
-        for b, width in enumerate((W, QUARTER)):
-            turned = psum.tile([P, width], F32, name="turned%d" % b, tag="bank%d" % (5 + b))
+        groups = ((0, 1, 6, 7), (2, 3, 4, 5))
+        turned_z = [keep.tile([P, 4, 2 * P], BF16, name="turned_z0"), placed([P, 4, 2 * P], BF16, "turned_z1", 1024)]
+        for s, terms, banks in ((0, (emb_sb[0], up_first, up[0]), (0, 1)), (1, (emb_sb[1], up[1]), (3, 4))):
+            for b, group in enumerate(groups):
+                total = psum.tile([P, 4, P], F32, name="total%d_%d" % (s, b), tag="bank%d" % banks[b])
+                for i, term in enumerate(terms):
+                    for n, block in enumerate(group):
+                        nc.tensor.matmul(
+                            total[:, n, :],
+                            lhsT=term[:, block * P : (block + 1) * P],
+                            rhs=ident[:],
+                            is_transpose=True,
+                            start=(i == 0 and n == 0),
+                            stop=(i == len(terms) - 1 and n == 3),
+                        )
+                nc.scalar.copy(turned_z[b][:, :, s * P : (s + 1) * P], total[:])
+        turned_sb = []
+        for name, lo, width, bank in (("a", 0, QUARTER, 6), ("m", QUARTER, 2 * QUARTER, 2)):
+            turned = psum.tile([P, width], F32, name="turned_" + name, tag="bank%d" % bank)
             for c in range(0, width, P):
-                nc.tensor.transpose(turned[:, c : c + P], emb_sb[3][:, b * W + c : b * W + c + P], ident[:])
-            turned_sb = keep.tile([P, width], F32, name="turned_sb%d" % b)
-            nc.scalar.copy(turned_sb[:], turned[:])
-            back = psum.tile([P, width], F32, name="emb_ps%d" % b, tag="bank%d" % (2 + b))
-            for c in range(0, width, P):
-                nc.tensor.transpose(back[:, c : c + P], turned_sb[:, c : c + P], ident[:])
-            emb_ps.append(back)
-        planes = [keep.tile([P, 3, W], BF16, name="planes%d" % b) for b in range(2)]
-        blocks = [planes[b][:].rearrange("p r (k c) -> p (r k) c", c=QUARTER) for b in range(2)]
-        for t in range(2):
-            width = W if t == 0 else QUARTER
-            for lo in (0, W) if t == 0 else (0, W, QUARTER, W + QUARTER):
-                z_half = keep.tile([P, width], BF16, name="z_half%d_%d" % (t, lo))
-                nc.gpsimd.tensor_tensor(z_half[:], up[t][:, lo : lo + width], (emb_first if t == 0 else emb_sb[t])[:, lo : lo + width], ADD)
-                nc.sync.dma_start(planes[lo // W][64 * t : 64 * (t + 1), 1:3, lo % W : lo % W + width], z_half[:])
-        stretches = ((0, 256), (256, 512), (512, 768), (768, U))
-        z_a, z_b, z_c, z_d = [keep.tile([P, hi - lo, PACK], BF16, name="z_bf%d" % lo, align_bytes=64) for lo, hi in stretches]
-        early = ((z_a[:], 0, 256), (z_c[:], 512, 768), (z_b[:], 256, 512), (z_d[:], 768, U))
-        pieces = (
-            (z_a[:, :64, :], 0, 64),
-            (z_a[:, 64:, :], 64, 256),
-            (z_b[:, :P, :], 256, 384),
-            (z_b[:, P:, :], 384, 512),
-            (z_c[:], 512, 768),
-        )
+                nc.tensor.transpose(turned[:, c : c + P], emb_sb[3][:, lo + c : lo + c + P], ident[:])
+            turned_sb.append(keep.tile([P, width], F32, name="turned_sb_" + name))
+            nc.scalar.copy(turned_sb[-1][:], turned[:])
 
-        nc.gpsimd.tensor_tensor(z_d[:, :, 2], up[2][:, 768:U], emb_sb[2][:, 768:U], ADD)
-        for z_bf, lo, hi in early:
-            src = planes[lo // W][:, 1:3, lo % W : lo % W + hi - lo]
-            nc.scalar.copy(z_bf[:, :, 0:2], src.rearrange("p e c -> p c e"))
-        for lo, hi in ((0, W), (W, 768)):
-            nc.gpsimd.tensor_tensor(planes[lo // W][:, 0, 0 : hi - lo], up[2][:, lo:hi], emb_sb[2][:, lo:hi], ADD)
-        nc.gpsimd.tensor_tensor(z_d[:, :, 3], up[3][:, 768:U], emb_sb[3][:, 768:U], ADD)
-        for lo, hi in ((0, 64), (64, 256), (256, 512), (512, 768)):
-            dst = blocks[lo // W][:, 3 + 2 * (lo // QUARTER % 2), lo % QUARTER : lo % QUARTER + hi - lo]
-            nc.vector.tensor_tensor(dst, up[3][:, lo:hi], emb_ps[lo // W][:, lo % W : lo % W + hi - lo], ADD)
-        for z_bf, lo, hi in pieces:
-            k = lo // QUARTER % 2
-            src = blocks[lo // W][:, k : 4 + 2 * k : 3 + k, lo % QUARTER : lo % QUARTER + hi - lo]
-            copy = nc.vector.tensor_copy if lo >= W else nc.scalar.copy
-            copy(z_bf[:, :, 2:4], src.rearrange("p e c -> p c e"))
+        def turn_back(src, bank, name):
+            back = psum.tile([P, src.shape[1]], F32, name=name, tag="bank%d" % bank)
+            for c in range(0, src.shape[1], P):
+                nc.tensor.transpose(back[:, c : c + P], src[:, c : c + P], ident[:])
+            return back
+
+        emb_a = turn_back(turned_sb[0][:], 6, "emb_a")
+        words = [turned_z[b][:].rearrange("p n h -> p (n h)").bitcast(F32) for b in range(2)]
+        z_bf = [keep.tile([P, QUARTER, PACK], BF16, name="z_bf%d" % k, align_bytes=64) for k in range(4)]
+
+        def z_words(k):
+            return z_bf[k][:].rearrange("p c t -> p (c t)").bitcast(F32).rearrange("p (c u) -> p c u", u=2)
+
+        for k, bank in ((0, 0), (3, 1)):
+            back = turn_back(words[0][:, k // 3 * QUARTER : (k // 3 + 1) * QUARTER], bank, "early%d" % k)
+            nc.scalar.copy(z_words(k)[:, :, 0], back[:])
+        early_mid = {k: turn_back(words[1][:, (k - 1) * QUARTER : k * QUARTER], bank, "early%d" % k) for k, bank in ((2, 5), (1, 2))}
+        rows = keep.tile([P, 3, QUARTER], BF16, name="rows")
+        plane2_dst = (rows[:, 0, :], rows[:, 1, :], rows[:, 2, :], z_bf[3][:, :, 2])
+        for k in (1, 2, 0, 3):
+            nc.gpsimd.tensor_tensor(plane2_dst[k], up[2][:, k * QUARTER : (k + 1) * QUARTER], emb_sb[2][:, k * QUARTER : (k + 1) * QUARTER], ADD)
+        nc.gpsimd.tensor_tensor(z_bf[3][:, :, 3], up[3][:, 768:U], emb_sb[3][:, 768:U], ADD)
+        pairs = {k: placed([P, 2, QUARTER, 2], BF16, "pairs%d" % k, 2048 * (k - 1)) for k in (1, 2)}
+
+        def first_words(k):
+            nc.scalar.copy(pairs[k][:, 0].rearrange("p c e -> p (c e)").bitcast(F32), early_mid[k][:])
+
+        first_words(2)
+        for k in (1, 2):
+            nc.scalar.copy(pairs[k][:, 1], rows[:, k, :].unsqueeze(2).to_broadcast([P, QUARTER, 2]))
+        first_words(1)
+        emb_mid = {k: turn_back(turned_sb[1][:, (k - 1) * QUARTER : k * QUARTER], bank, "emb_mid%d" % k) for k, bank in ((2, 5), (1, 2))}
+        for lo, hi in ((0, 64), (64, QUARTER)):
+            nc.vector.tensor_tensor(rows[:, 2, lo:hi], up[3][:, lo:hi], emb_a[:, lo:hi], ADD)
+        for k in (2, 1):
+            nc.vector.tensor_tensor(pairs[k][:, 1, :, 1], up[3][:, k * QUARTER : (k + 1) * QUARTER], emb_mid[k][:], ADD)
+        for lo, hi in ((0, 64), (64, QUARTER)):
+            nc.scalar.copy(z_bf[0][:, lo:hi, 2:4], rows[:, 0:3:2, lo:hi].rearrange("p e c -> p c e"))
+
+        def weave(k, lo, hi):
+            src = pairs[k][:].rearrange("p u c e -> p u (c e)").bitcast(U32)[:, :, lo:hi]
+            dst = z_bf[k][:, lo:hi, :].rearrange("p c t -> p (c t)").bitcast(U32).rearrange("p (c u) -> p c u", u=2)
+            nc.scalar.copy(dst, src.rearrange("p u c -> p c u"))
+
+        weave(2, 0, QUARTER)
+        weave(1, 0, P)
+        weave(1, P, QUARTER)
+        z_a, z_b, z_c, z_d = z_bf
 
         y = keep.tile([P, U], F32, name="y")
         chunks = [
@@ -236,10 +263,10 @@ def tile_picked_devox_none_p_kernel(
         ]
         accs = []
         for n, (z_bf, lo, hi, copy) in enumerate(chunks):
-            z_codes = keep.tile([P, hi - lo], U32, name="z_codes%d" % n, align_bytes=64)
+            z_codes = placed([P, hi - lo], U32, "z_codes%d" % n, 8192 + 2048 * n)
             z_sc = keep.tile([P, hi - lo], U8, name="z_sc%d" % n, align_bytes=64)
             nc.vector.quantize_mx(z_codes[:].bitcast(FP8X4), z_sc[:], z_bf.rearrange("p c t -> p (c t)"))
-            y_acc = psum.tile([P, hi - lo], F32, name="y_acc%d" % n, tag="bank%d" % ((5 + n) % 8))
+            y_acc = psum.tile([P, hi - lo], F32, name="y_acc%d" % n, tag="bank%d" % (7, 3, 4, 0, 1)[n])
             nc.tensor.matmul_mx(
                 y_acc[:],
                 lhsT=w2_codes[:].bitcast(FP4X4),

@@ -47,8 +47,10 @@ def tile_picked_devox_none_p_kernel(
         up.append(laid.tile([P, U], F32, name="up3", offset=8192, align_bytes=64))
         up_first = keep.tile([P, U], F32, name="up_first")
         nc.vector.memset(up_first[:], 0.0)
+        up_second = keep.tile([P, U], F32, name="up_second")
         for t in range(PACK):
             (nc.vector if t < 2 else nc.gpsimd).memset(up[t][:], 0.0)
+        nc.gpsimd.memset(up_second[:], 0.0)
 
         def staged(shape, dtype, name, slot):
             return keep.tile(shape, dtype, name=name, tag=slot, align_bytes=64)
@@ -165,7 +167,7 @@ def tile_picked_devox_none_p_kernel(
         for d in range(2):
             gate_sb.append(staged([P, V], F32, "gate_sb%d" % d, "high1_0" if d == 0 else "raw1"))
             nc.sync.dma_start(gate_sb[d][:], gate[d])
-        first_product(0, HALF, S, 2, h_last[:])
+        first_product(0, HALF, S, 0, h_last[:])
         scatter(0, HALF, S, h_last[:])
         w2_sc = staged([P, N], U8, "w2_sc", "high0_0")
         nc.gpsimd.memset(w2_sc[:].bitcast(I32), 0)
@@ -173,7 +175,8 @@ def tile_picked_devox_none_p_kernel(
             nc.sync.dma_start(w2_sc[32 * q : 32 * q + 4, :].bitcast(I32), w2_scales[0, 4 * q : 4 * q + 4, :].bitcast(I32))
         for a in range(2):
             first_product(1, a * HALF, (a + 1) * HALF, 3 + a, h[1][:, a * HALF : (a + 1) * HALF])
-        scatter(1, 0, S, h[1][:])
+        nc.vector.tensor_copy(up_second[:].indirect(cell_sb[:, 0 : HALF // 16]), h[1][:, 0:HALF])
+        scatter(1, HALF, S, h[1][:, HALF:S])
         for t in range(2, PACK):
             first_product(t, 0, S, 1 + t, h[t][:])
             scatter(t, 0, S, h[t][:])
@@ -182,7 +185,7 @@ def tile_picked_devox_none_p_kernel(
         make_identity(nc, ident[:])
         groups = ((0, 1, 6, 7), (2, 3, 4, 5))
         turned_z = [keep.tile([P, 4, 2 * P], BF16, name="turned_z0"), placed([P, 4, 2 * P], BF16, "turned_z1", 1024)]
-        for s, terms, banks in ((0, (emb_sb[0], up_first, up[0]), (0, 1)), (1, (emb_sb[1], up[1]), (3, 4))):
+        for s, terms, banks in ((0, (emb_sb[0], up_first, up[0]), (0, 1)), (1, (emb_sb[1], up_second, up[1]), (3, 4))):
             for b, group in enumerate(groups):
                 total = psum.tile([P, 4, P], F32, name="total%d_%d" % (s, b), tag="bank%d" % banks[b])
                 for i, term in enumerate(terms):

@@ -39,18 +39,15 @@ def tile_picked_devox_none_p_kernel(
             nc.sync.dma_start(tile[:], src)
             return tile
 
-        xs_all = keep.tile([P, T], U8, name="xs_all", align_bytes=64)
+        xs_all = laid.tile([P, T], U8, name="xs_all", offset=8192, align_bytes=64)
         xs_mm = keep.tile([P, PASSES, S], U8, name="xs_mm", align_bytes=64)
         nc.gpsimd.memset(xs_all[:].bitcast(I32), 0)
         nc.vector.memset(xs_mm[:].bitcast(I32), 0)
-        up = [keep.tile([P, U], F32, name="up%d" % t) for t in range(PACK - 1)]
-        up.append(laid.tile([P, U], F32, name="up3", offset=8192, align_bytes=64))
+        up = [keep.tile([P, U], F32, name="up%d" % t) for t in range(2)]
         up_first = keep.tile([P, U], F32, name="up_first")
-        nc.vector.memset(up_first[:], 0.0)
         up_second = keep.tile([P, U], F32, name="up_second")
-        for t in range(PACK):
-            (nc.vector if t < 2 else nc.gpsimd).memset(up[t][:], 0.0)
-        nc.gpsimd.memset(up_second[:], 0.0)
+        for window in (up_first, up[0], up_second, up[1]):
+            nc.vector.memset(window[:], 0.0)
 
         def staged(shape, dtype, name, slot):
             return keep.tile(shape, dtype, name=name, tag=slot, align_bytes=64)
@@ -110,6 +107,10 @@ def tile_picked_devox_none_p_kernel(
         xw_pick = [keep.tile([P, S], U32, name="xw_pick%d" % g, align_bytes=64) for g in range(PASSES)]
         rounded = round_w1(0, 0)
         nc.vector.tensor_copy(xs_pick[:], xs_all[:].indirect(offs_sb[:]))
+        up.append(staged([P, U], F32, "up2", "raw0"))
+        up.append(placed([P, U], F32, "up3", 8192))
+        for t in (2, 3):
+            nc.gpsimd.memset(up[t][:], 0.0)
         for q in (0, 2, 1, 3):
             nc.sync.dma_start(xs_mm[32 * q : 32 * q + 4].bitcast(I32), xs_pick[32 * q : 32 * q + 32 : 4, :].bitcast(I32))
         pack_w1(0, 0, *rounded)

@@ -39,13 +39,13 @@ def tile_picked_devox_none_p_kernel(
             nc.sync.dma_start(tile[:], src)
             return tile
 
-        xs_all = laid.tile([P, T], U8, name="xs_all", offset=8192, align_bytes=64)
+        xs_all = keep.tile([P, T], U8, name="xs_all", align_bytes=64)
         xs_mm = keep.tile([P, PASSES, S], U8, name="xs_mm", align_bytes=64)
         nc.gpsimd.memset(xs_all[:].bitcast(I32), 0)
         nc.vector.memset(xs_mm[:].bitcast(I32), 0)
         up = [keep.tile([P, U], F32, name="up%d" % t) for t in range(2)]
         up_first = keep.tile([P, U], F32, name="up_first")
-        up_second = keep.tile([P, U], F32, name="up_second")
+        up_second = laid.tile([P, U], F32, name="up_second", offset=8192, align_bytes=64)
         for window in (up_first, up[0], up_second, up[1]):
             nc.vector.memset(window[:], 0.0)
 
@@ -54,6 +54,9 @@ def tile_picked_devox_none_p_kernel(
 
         def placed(shape, dtype, name, offset):
             return laid.tile(shape, dtype, name=name, offset=offset, align_bytes=64)
+
+        ident = keep.tile([P, P], F32, name="ident")
+        make_identity(nc, ident[:])
 
         w1_rows = w1.rearrange("(g p j) (hf c) -> hf g p j c", p=P, j=PACK, hf=2)
         raw = [[None, None], [None, None]]
@@ -108,9 +111,7 @@ def tile_picked_devox_none_p_kernel(
         rounded = round_w1(0, 0)
         nc.vector.tensor_copy(xs_pick[:], xs_all[:].indirect(offs_sb[:]))
         up.append(staged([P, U], F32, "up2", "raw0"))
-        up.append(placed([P, U], F32, "up3", 8192))
-        for t in (2, 3):
-            nc.gpsimd.memset(up[t][:], 0.0)
+        nc.gpsimd.memset(up[2][:], 0.0)
         for q in (0, 2, 1, 3):
             nc.sync.dma_start(xs_mm[32 * q : 32 * q + 4].bitcast(I32), xs_pick[32 * q : 32 * q + 32 : 4, :].bitcast(I32))
         pack_w1(0, 0, *rounded)
@@ -133,7 +134,7 @@ def tile_picked_devox_none_p_kernel(
                 xw_pick[1][:, a * HALF : (a + 1) * HALF], xw_all[1][:].indirect(offs_sb[:, 16 * a : 16 * (a + 1)])
             )
 
-        h = [keep.tile([P, S], F32, name="h%d" % t) for t in range(PACK)]
+        h = [staged([P, S], F32, "h%d" % t, "h%d" % t) for t in range(PACK)]
 
         def first_product(t, lo, hi, bank, dst):
             acc = psum.tile([P, hi - lo], F32, name="acc%d_%d" % (t, lo), tag="bank%d" % bank)
@@ -168,6 +169,14 @@ def tile_picked_devox_none_p_kernel(
         for d in range(2):
             gate_sb.append(staged([P, V], F32, "gate_sb%d" % d, "high1_0" if d == 0 else "raw1"))
             nc.sync.dma_start(gate_sb[d][:], gate[d])
+
+        def add_window(dst, window, rows):
+            for quarters in (slice(0, 4, 3), slice(1, 3)):
+                views = [x[:].rearrange("p (k c) -> p k c", c=QUARTER)[:, quarters, :] for x in (dst, window, rows)]
+                nc.gpsimd.tensor_tensor(*views, ADD)
+
+        emb_first = staged([P, U], F32, "emb_first", "high1_1")
+        add_window(emb_first, up_first, emb_sb[0])
         first_product(0, HALF, S, 0, h_last[:])
         scatter(0, HALF, S, h_last[:])
         w2_sc = staged([P, N], U8, "w2_sc", "high0_0")
@@ -177,16 +186,18 @@ def tile_picked_devox_none_p_kernel(
         for a in range(2):
             first_product(1, a * HALF, (a + 1) * HALF, 3 + a, h[1][:, a * HALF : (a + 1) * HALF])
         nc.vector.tensor_copy(up_second[:].indirect(cell_sb[:, 0 : HALF // 16]), h[1][:, 0:HALF])
+        emb_second = keep.tile([P, U], F32, name="emb_second")
+        add_window(emb_second, up_second, emb_sb[1])
+        up.append(placed([P, U], F32, "up3", 8192))
+        nc.gpsimd.memset(up[3][:], 0.0)
         scatter(1, HALF, S, h[1][:, HALF:S])
         for t in range(2, PACK):
             first_product(t, 0, S, 1 + t, h[t][:])
             scatter(t, 0, S, h[t][:])
 
-        ident = staged([P, P], F32, "ident", "high1_1")
-        make_identity(nc, ident[:])
         groups = ((0, 1, 6, 7), (2, 3, 4, 5))
         turned_z = [keep.tile([P, 4, 2 * P], BF16, name="turned_z0"), placed([P, 4, 2 * P], BF16, "turned_z1", 1024)]
-        for s, terms, banks in ((0, (emb_sb[0], up_first, up[0]), (0, 1)), (1, (emb_sb[1], up_second, up[1]), (3, 4))):
+        for s, terms, banks in ((0, (emb_first, up[0]), (0, 1)), (1, (up[1], emb_second), (3, 4))):
             for b, group in enumerate(groups):
                 total = psum.tile([P, 4, P], F32, name="total%d_%d" % (s, b), tag="bank%d" % banks[b])
                 for i, term in enumerate(terms):

@@ -183,21 +183,21 @@ def tile_picked_devox_none_p_kernel(
         nc.gpsimd.memset(w2_sc[:].bitcast(I32), 0)
         for q in range(4):
             nc.sync.dma_start(w2_sc[32 * q : 32 * q + 4, :].bitcast(I32), w2_scales[0, 4 * q : 4 * q + 4, :].bitcast(I32))
-        for a in range(2):
-            first_product(1, a * HALF, (a + 1) * HALF, 3 + a, h[1][:, a * HALF : (a + 1) * HALF])
-        nc.vector.tensor_copy(up_second[:].indirect(cell_sb[:, 0 : HALF // 16]), h[1][:, 0:HALF])
+        for lo, hi, bank in ((0, P, 3), (P, P + HALF, 7), (P + HALF, S, 4)):
+            first_product(1, lo, hi, bank, h[1][:, lo:hi])
+        nc.vector.tensor_copy(up_second[:].indirect(cell_sb[:, 0 : P // 16]), h[1][:, 0:P])
         emb_second = keep.tile([P, U], F32, name="emb_second")
         add_window(emb_second, up_second, emb_sb[1])
         up.append(placed([P, U], F32, "up3", 8192))
         nc.gpsimd.memset(up[3][:], 0.0)
-        scatter(1, HALF, S, h[1][:, HALF:S])
+        scatter(1, P, S, h[1][:, P:S])
         for t in range(2, PACK):
             first_product(t, 0, S, 1 + t, h[t][:])
             scatter(t, 0, S, h[t][:])
 
         groups = ((0, 1, 6, 7), (2, 3, 4, 5))
         turned_z = [keep.tile([P, 4, 2 * P], BF16, name="turned_z0"), placed([P, 4, 2 * P], BF16, "turned_z1", 1024)]
-        for s, terms, banks in ((0, (emb_first, up[0]), (0, 1)), (1, (up[1], emb_second), (3, 4))):
+        for s, terms, banks in ((0, (emb_first, up[0]), (0, 1)), (1, (emb_second, up[1]), (3, 4))):
             for b, group in enumerate(groups):
                 total = psum.tile([P, 4, P], F32, name="total%d_%d" % (s, b), tag="bank%d" % banks[b])
                 for i, term in enumerate(terms):

@@ -46,8 +46,10 @@ def tile_picked_devox_none_p_kernel(
         up = [keep.tile([P, U], F32, name="up%d" % t) for t in range(2)]
         up_first = keep.tile([P, U], F32, name="up_first")
         up_second = laid.tile([P, U], F32, name="up_second", offset=8192, align_bytes=64)
+        zero = keep.tile([P, 8], F32, name="zero")
+        nc.vector.memset(zero[:], 0.0)
         for window in (up_first, up[0], up_second, up[1]):
-            nc.vector.memset(window[:], 0.0)
+            nc.scalar.copy(window[:], zero[:, 0:1].to_broadcast([P, U]))
 
         def staged(shape, dtype, name, slot):
             return keep.tile(shape, dtype, name=name, tag=slot, align_bytes=64)
@@ -92,7 +94,7 @@ def tile_picked_devox_none_p_kernel(
             high_dst = high[:].rearrange("p (e m j) -> p m e j", e=2, j=PACK)
             if hf == 0:
                 nc.vector.tensor_copy(low_dst, src[:, :, 0:2, :])
-                nc.scalar.copy(high_dst, src[:, :, 2:4, :])
+                nc.vector.tensor_copy(high_dst, src[:, :, 2:4, :])
             else:
                 nc.scalar.copy(low_dst, src[:, :, 0:2, :])
                 nc.gpsimd.tensor_scalar(high_dst, src[:, :, 2:4, :], 1.0, 0.0, MULT, ADD)
@@ -110,8 +112,8 @@ def tile_picked_devox_none_p_kernel(
         xw_pick = [keep.tile([P, S], U32, name="xw_pick%d" % g, align_bytes=64) for g in range(PASSES)]
         rounded = round_w1(0, 0)
         nc.vector.tensor_copy(xs_pick[:], xs_all[:].indirect(offs_sb[:]))
-        up.append(staged([P, U], F32, "up2", "raw0"))
-        nc.gpsimd.memset(up[2][:], 0.0)
+        up.append(keep.tile([P, U], F32, name="up2"))
+        nc.scalar.copy(up[2][:], zero[:, 0:1].to_broadcast([P, U]))
         for q in (0, 2, 1, 3):
             nc.sync.dma_start(xs_mm[32 * q : 32 * q + 4].bitcast(I32), xs_pick[32 * q : 32 * q + 32 : 4, :].bitcast(I32))
         pack_w1(0, 0, *rounded)

@@ -198,7 +198,7 @@ def tile_picked_devox_none_p_kernel(
             scatter(t, 0, S, h[t][:])
 
         groups = ((0, 1, 6, 7), (2, 3, 4, 5))
-        turned_z = [keep.tile([P, 4, 2 * P], BF16, name="turned_z0"), placed([P, 4, 2 * P], BF16, "turned_z1", 1024)]
+        turned_z = [keep.tile([P, 4, 2 * P], BF16, name="turned_z0"), placed([P, 4, 2 * P], BF16, "turned_z1", 1536)]
         for s, terms, banks in ((0, (emb_first, up[0]), (0, 1)), (1, (emb_second, up[1]), (3, 4))):
             for b, group in enumerate(groups):
                 total = psum.tile([P, 4, P], F32, name="total%d_%d" % (s, b), tag="bank%d" % banks[b])
@@ -229,52 +229,72 @@ def tile_picked_devox_none_p_kernel(
 
         emb_a = turn_back(turned_sb[0][:], 6, "emb_a")
         words = [turned_z[b][:].rearrange("p n h -> p (n h)").bitcast(F32) for b in range(2)]
-        z_bf = [keep.tile([P, QUARTER, PACK], BF16, name="z_bf%d" % k, align_bytes=64) for k in range(4)]
+        z_a = keep.tile([P, QUARTER, PACK], BF16, name="z_a", align_bytes=64)
+        z_b = keep.tile([P, QUARTER, PACK], BF16, name="z_b", align_bytes=64)
+        z_cd = keep.tile([P, 2 * QUARTER, PACK], BF16, name="z_cd", align_bytes=64)
+        DIRECT = 320
+        PAIRED = 2 * QUARTER - DIRECT
 
-        def z_words(k):
-            return z_bf[k][:].rearrange("p c t -> p (c t)").bitcast(F32).rearrange("p (c u) -> p c u", u=2)
+        def z_words(z):
+            return z.rearrange("p c t -> p (c t)").bitcast(F32).rearrange("p (c u) -> p c u", u=2)
 
-        for k, bank in ((0, 0), (3, 1)):
-            back = turn_back(words[0][:, k // 3 * QUARTER : (k // 3 + 1) * QUARTER], bank, "early%d" % k)
-            nc.scalar.copy(z_words(k)[:, :, 0], back[:])
+        pairs = {
+            1: placed([P, 2, QUARTER, 2], BF16, "pairs1", 0),
+            2: placed([P, 2, PAIRED, 2], BF16, "pairs2", 3072),
+            0: placed([P, 2, P, 2], BF16, "pairs0", 2048),
+        }
+
+        def first_words(k, src):
+            nc.scalar.copy(pairs[k][:, 0].rearrange("p c e -> p (c e)").bitcast(F32), src)
+
+        early0 = turn_back(words[0][:, 0:QUARTER], 0, "early0")
+        nc.scalar.copy(z_words(z_a[:, 0:P, :])[:, :, 0], early0[:, 0:P])
+        early3 = turn_back(words[0][:, QUARTER : 2 * QUARTER], 1, "early3")
+        nc.scalar.copy(z_words(z_cd[:, QUARTER:, :])[:, :, 0], early3[:])
         early_mid = {k: turn_back(words[1][:, (k - 1) * QUARTER : k * QUARTER], bank, "early%d" % k) for k, bank in ((2, 5), (1, 2))}
-        rows = keep.tile([P, 3, QUARTER], BF16, name="rows")
-        plane2_dst = (rows[:, 0, :], rows[:, 1, :], rows[:, 2, :], z_bf[3][:, :, 2])
-        for k in (1, 2, 0, 3):
-            nc.gpsimd.tensor_tensor(plane2_dst[k], up[2][:, k * QUARTER : (k + 1) * QUARTER], emb_sb[2][:, k * QUARTER : (k + 1) * QUARTER], ADD)
-        nc.gpsimd.tensor_tensor(z_bf[3][:, :, 3], up[3][:, 768:U], emb_sb[3][:, 768:U], ADD)
-        pairs = {k: placed([P, 2, QUARTER, 2], BF16, "pairs%d" % k, 2048 * (k - 1)) for k in (1, 2)}
+        first_words(0, early0[:, P:QUARTER])
+        nc.scalar.copy(z_words(z_cd[:, PAIRED:QUARTER, :])[:, :, 0], early_mid[2][:, PAIRED:QUARTER])
+        rows = keep.tile([P, 2, P], BF16, name="rows")
+        spans = {0: (P, QUARTER), 1: (QUARTER, 2 * QUARTER), 2: (2 * QUARTER, U - DIRECT)}
+        middle = keep.tile([P, QUARTER + PAIRED], BF16, name="middle")
+        plane2 = {0: rows[:, 1, :], 1: middle[:, 0:QUARTER], 2: middle[:, QUARTER:]}
+        nc.gpsimd.tensor_tensor(middle[:], up[2][:, QUARTER : U - DIRECT], emb_sb[2][:, QUARTER : U - DIRECT], ADD)
+        nc.gpsimd.tensor_tensor(rows[:].rearrange("p e c -> p (e c)"), up[2][:, 0:QUARTER], emb_sb[2][:, 0:QUARTER], ADD)
+        nc.gpsimd.tensor_tensor(z_cd[:, PAIRED:, 2], up[2][:, U - DIRECT : U], emb_sb[2][:, U - DIRECT : U], ADD)
+        nc.gpsimd.tensor_tensor(z_cd[:, PAIRED:, 3], up[3][:, U - DIRECT : U], emb_sb[3][:, U - DIRECT : U], ADD)
 
-        def first_words(k):
-            nc.scalar.copy(pairs[k][:, 0].rearrange("p c e -> p (c e)").bitcast(F32), early_mid[k][:])
-
-        first_words(2)
-        for k in (1, 2):
-            nc.scalar.copy(pairs[k][:, 1], rows[:, k, :].unsqueeze(2).to_broadcast([P, QUARTER, 2]))
-        first_words(1)
+        first_words(2, early_mid[2][:, 0:PAIRED])
+        for k in (1, 2, 0):
+            lo, hi = spans[k]
+            nc.scalar.copy(pairs[k][:, 1], plane2[k].unsqueeze(2).to_broadcast([P, hi - lo, 2]))
+        first_words(1, early_mid[1][:])
         emb_mid = {k: turn_back(turned_sb[1][:, (k - 1) * QUARTER : k * QUARTER], bank, "emb_mid%d" % k) for k, bank in ((2, 5), (1, 2))}
-        for lo, hi in ((0, 64), (64, QUARTER)):
-            nc.vector.tensor_tensor(rows[:, 2, lo:hi], up[3][:, lo:hi], emb_a[:, lo:hi], ADD)
-        for k in (2, 1):
-            nc.vector.tensor_tensor(pairs[k][:, 1, :, 1], up[3][:, k * QUARTER : (k + 1) * QUARTER], emb_mid[k][:], ADD)
-        for lo, hi in ((0, 64), (64, QUARTER)):
-            nc.scalar.copy(z_bf[0][:, lo:hi, 2:4], rows[:, 0:3:2, lo:hi].rearrange("p e c -> p c e"))
+        nc.vector.tensor_tensor(rows[:, 1, :], up[3][:, 0:P], emb_a[:, 0:P], ADD)
+        for k, emb_turned in ((0, emb_a[:, P:QUARTER]), (2, emb_mid[2][:, 0:PAIRED]), (1, emb_mid[1][:])):
+            lo, hi = spans[k]
+            nc.vector.tensor_tensor(pairs[k][:, 1, :, 1], up[3][:, lo:hi], emb_turned, ADD)
+        nc.scalar.copy(z_a[:, 0:P, 2:4], rows[:].rearrange("p e c -> p c e"))
 
-        def weave(k, lo, hi):
+        def weave(copy, k, lo, hi, z):
             src = pairs[k][:].rearrange("p u c e -> p u (c e)").bitcast(U32)[:, :, lo:hi]
-            dst = z_bf[k][:, lo:hi, :].rearrange("p c t -> p (c t)").bitcast(U32).rearrange("p (c u) -> p c u", u=2)
-            nc.scalar.copy(dst, src.rearrange("p u c -> p c u"))
+            dst = z.rearrange("p c t -> p (c t)").bitcast(U32).rearrange("p (c u) -> p c u", u=2)
+            if copy is nc.vector:
+                copy.tensor_copy(dst.bitcast(I32), src.rearrange("p u c -> p c u").bitcast(I32))
+            else:
+                copy.copy(dst, src.rearrange("p u c -> p c u"))
 
-        weave(2, 0, QUARTER)
-        weave(1, 0, P)
-        weave(1, P, QUARTER)
-        z_a, z_b, z_c, z_d = z_bf
+        weave(nc.scalar, 0, 0, P, z_a[:, P:QUARTER, :])
+        weave(nc.vector, 2, P, PAIRED, z_cd[:, P:PAIRED, :])
+        weave(nc.scalar, 2, 0, P, z_cd[:, 0:P, :])
+        weave(nc.scalar, 1, 0, P, z_b[:, 0:P, :])
+        weave(nc.scalar, 1, P, QUARTER, z_b[:, P:QUARTER, :])
+        z_c, z_d = z_cd[:, 0:QUARTER, :], z_cd[:, QUARTER:, :]
 
         y = keep.tile([P, U], F32, name="y")
         chunks = [
-            (z_d[:], 768, U, nc.scalar.copy),
+            (z_d, 768, U, nc.scalar.copy),
             (z_a[:], 0, 256, nc.scalar.copy),
-            (z_c[:], 512, 768, nc.vector.tensor_copy),
+            (z_c, 512, 768, nc.vector.tensor_copy),
             (z_b[:, :P, :], 256, 384, nc.vector.tensor_copy),
             (z_b[:, P:, :], 384, 512, nc.scalar.copy),
         ]

@@ -131,10 +131,8 @@ def tile_picked_devox_none_p_kernel(
 
         load_emb(0, "low0_1")
         load_emb(1, "high0_1")
-        for a in range(2):
-            nc.vector.tensor_copy(
-                xw_pick[1][:, a * HALF : (a + 1) * HALF], xw_all[1][:].indirect(offs_sb[:, 16 * a : 16 * (a + 1)])
-            )
+        for lo, hi in ((0, P), (P, HALF), (HALF, S)):
+            nc.vector.tensor_copy(xw_pick[1][:, lo:hi], xw_all[1][:].indirect(offs_sb[:, lo // 16 : hi // 16]))
 
         h = [staged([P, S], F32, "h%d" % t, "h%d" % t) for t in range(PACK)]
 

@@ -64,8 +64,9 @@ def tile_picked_devox_none_p_kernel(
         raw = [[None, None], [None, None]]
 
         def load_w1(hf, g, slot):
-            raw[hf][g] = staged([P, PACK, H // 2], F32, "raw%d_%d" % (hf, g), slot)
-            nc.sync.dma_start(raw[hf][g][:], w1_rows[hf, g])
+            tile = staged([P, PACK, H // 2], F32, "raw%d_%d" % (hf, g), slot)
+            raw[hf][g] = tile[:]
+            nc.sync.dma_start(tile[:], w1_rows[hf, g])
 
         xw_all = [keep.tile([P, T], U32, name="xw_all%d" % g) for g in range(PASSES)]
         x_rows = x_words.rearrange("g p n t -> g p (n t)").bitcast(I32)
@@ -87,7 +88,7 @@ def tile_picked_devox_none_p_kernel(
             nc.vector.quantize_mx(w1_codes[g][:, cols].bitcast(FP8X4), w1_sc[g][:, cols], src)
 
         def round_w1(hf, g):
-            src = raw[hf][g][:].rearrange("p j (m t) -> p m t j", t=PACK)
+            src = raw[hf][g].rearrange("p j (m t) -> p m t j", t=PACK)
             low = staged([P, H], BF16, "low%d_%d" % (hf, g), "low%d_%d" % (hf, g))
             high = staged([P, H], BF16, "high%d_%d" % (hf, g), "high%d_%d" % (hf, g))
             low_dst = low[:].rearrange("p (m e j) -> p m e j", e=2, j=PACK)
@@ -95,9 +96,12 @@ def tile_picked_devox_none_p_kernel(
             if hf == 0:
                 nc.vector.tensor_copy(low_dst, src[:, :, 0:2, :])
                 nc.vector.tensor_copy(high_dst, src[:, :, 2:4, :])
-            else:
+            elif g == 0:
                 nc.scalar.copy(low_dst, src[:, :, 0:2, :])
                 nc.gpsimd.tensor_scalar(high_dst, src[:, :, 2:4, :], 1.0, 0.0, MULT, ADD)
+            else:
+                nc.scalar.copy(low_dst, src[:, :, 0:2, :])
+                nc.scalar.copy(high_dst, src[:, :, 2:4, :])
             return low, high
 
         def pack_w1(hf, g, low, high):
@@ -118,7 +122,9 @@ def tile_picked_devox_none_p_kernel(
             nc.sync.dma_start(xs_mm[32 * q : 32 * q + 4].bitcast(I32), xs_pick[32 * q : 32 * q + 32 : 4, :].bitcast(I32))
         pack_w1(0, 0, *rounded)
         load_w1(1, 0, "low0_0")
-        load_w1(1, 1, "high0_0")
+        late = staged([P, S - P + PACK * HALF], F32, "late", "high0_0")
+        raw[1][1] = late[:, S - P :].rearrange("p (j c) -> p j c", j=PACK)
+        nc.sync.dma_start(raw[1][1], w1_rows[1, 1])
         nc.vector.tensor_copy(xw_pick[0][:], xw_all[0][:].indirect(offs_sb[:]))
         prepare_w1(0, 1)
         emb_half = emb.rearrange("(hf m t) c -> hf m t c", hf=2, t=PACK)
@@ -134,7 +140,9 @@ def tile_picked_devox_none_p_kernel(
         for lo, hi in ((0, P), (P, HALF), (HALF, S)):
             nc.vector.tensor_copy(xw_pick[1][:, lo:hi], xw_all[1][:].indirect(offs_sb[:, lo // 16 : hi // 16]))
 
-        h = [staged([P, S], F32, "h%d" % t, "h%d" % t) for t in range(PACK)]
+        h = {t: staged([P, S], F32, "h%d" % t, "h%d" % t) for t in (2, 3)}
+        h[0], h[1] = late[:, 0:S], late[:, S : 2 * S]
+        CUT = 384
 
         def first_product(t, lo, hi, bank, dst):
             acc = psum.tile([P, hi - lo], F32, name="acc%d_%d" % (t, lo), tag="bank%d" % bank)
@@ -156,19 +164,16 @@ def tile_picked_devox_none_p_kernel(
 
         first_product(0, 0, P, 0, h[0][:, 0:P])
         first_product(0, P, HALF, 1, h[0][:, P:HALF])
+        first_product(0, HALF, S - P, 0, h[0][:, HALF : S - P])
         nc.vector.tensor_copy(up_first[:].indirect(cell_sb[:, 0 : P // 16]), h[0][:, 0:P])
         scatter(0, P, HALF, h[0][:, P:HALF])
+        nc.vector.tensor_copy(up_first[:].indirect(cell_sb[:, HALF // 16 : CUT // 16]), h[0][:, HALF:CUT])
         prepare_w1(1, 0)
         prepare_w1(1, 1)
-        h_last = staged([P, HALF], F32, "h_last", "high0_0")
-        load_emb(2, "low0_0")
-        load_emb(3, "low1_0")
+        load_emb(2, "low1_0")
+        load_emb(3, "low0_0")
         w2_codes = staged([P, 2 * N], U8, "w2_codes", "low1_1")
         nc.sync.dma_start(w2_codes[:].bitcast(I32), w2_words[0].bitcast(I32))
-        gate_sb = []
-        for d in range(2):
-            gate_sb.append(staged([P, V], F32, "gate_sb%d" % d, "high1_0" if d == 0 else "raw1"))
-            nc.sync.dma_start(gate_sb[d][:], gate[d])
 
         def add_window(dst, window, rows):
             for quarters in (slice(0, 4, 3), slice(1, 3)):
@@ -177,13 +182,13 @@ def tile_picked_devox_none_p_kernel(
 
         emb_first = staged([P, U], F32, "emb_first", "high1_1")
         add_window(emb_first, up_first, emb_sb[0])
-        first_product(0, HALF, S, 0, h_last[:])
-        scatter(0, HALF, S, h_last[:])
-        w2_sc = staged([P, N], U8, "w2_sc", "high0_0")
+        first_product(0, S - P, S, 1, h[0][:, S - P : S])
+        scatter(0, CUT, S, h[0][:, CUT:S])
+        w2_sc = staged([P, N], U8, "w2_sc", "high1_0")
         nc.gpsimd.memset(w2_sc[:].bitcast(I32), 0)
         for q in range(4):
             nc.sync.dma_start(w2_sc[32 * q : 32 * q + 4, :].bitcast(I32), w2_scales[0, 4 * q : 4 * q + 4, :].bitcast(I32))
-        for lo, hi, bank in ((0, P, 3), (P, P + HALF, 7), (P + HALF, S, 4)):
+        for lo, hi, bank in ((0, P, 3), (P, HALF, 7), (HALF, S, 1)):
             first_product(1, lo, hi, bank, h[1][:, lo:hi])
         nc.vector.tensor_copy(up_second[:].indirect(cell_sb[:, 0 : P // 16]), h[1][:, 0:P])
         emb_second = keep.tile([P, U], F32, name="emb_second")
@@ -192,12 +197,16 @@ def tile_picked_devox_none_p_kernel(
         nc.gpsimd.memset(up[3][:], 0.0)
         scatter(1, P, S, h[1][:, P:S])
         for t in range(2, PACK):
-            first_product(t, 0, S, 1 + t, h[t][:])
+            first_product(t, 0, S, (3, 1)[t - 2], h[t][:])
             scatter(t, 0, S, h[t][:])
+        gate_sb = []
+        for d in range(2):
+            gate_sb.append(staged([P, V], F32, "gate_sb%d" % d, "h2" if d == 0 else "raw1"))
+            nc.sync.dma_start(gate_sb[d][:], gate[d])
 
         groups = ((0, 1, 6, 7), (2, 3, 4, 5))
         turned_z = [keep.tile([P, 4, 2 * P], BF16, name="turned_z0"), placed([P, 4, 2 * P], BF16, "turned_z1", 1536)]
-        for s, terms, banks in ((0, (emb_first, up[0]), (0, 1)), (1, (emb_second, up[1]), (3, 4))):
+        for s, terms, banks in ((0, (emb_first, up[0]), (0, 4)), (1, (emb_second, up[1]), (3, 1))):
             for b, group in enumerate(groups):
                 total = psum.tile([P, 4, P], F32, name="total%d_%d" % (s, b), tag="bank%d" % banks[b])
                 for i, term in enumerate(terms):
@@ -247,7 +256,7 @@ def tile_picked_devox_none_p_kernel(
 
         early0 = turn_back(words[0][:, 0:QUARTER], 0, "early0")
         nc.scalar.copy(z_words(z_a[:, 0:P, :])[:, :, 0], early0[:, 0:P])
-        early3 = turn_back(words[0][:, QUARTER : 2 * QUARTER], 1, "early3")
+        early3 = turn_back(words[0][:, QUARTER : 2 * QUARTER], 4, "early3")
         nc.scalar.copy(z_words(z_cd[:, QUARTER:, :])[:, :, 0], early3[:])
         early_mid = {k: turn_back(words[1][:, (k - 1) * QUARTER : k * QUARTER], bank, "early%d" % k) for k, bank in ((2, 5), (1, 2))}
         first_words(0, early0[:, P:QUARTER])
@@ -301,7 +310,7 @@ def tile_picked_devox_none_p_kernel(
             z_codes = placed([P, hi - lo], U32, "z_codes%d" % n, 8192 + 2048 * n)
             z_sc = keep.tile([P, hi - lo], U8, name="z_sc%d" % n, align_bytes=64)
             nc.vector.quantize_mx(z_codes[:].bitcast(FP8X4), z_sc[:], z_bf.rearrange("p c t -> p (c t)"))
-            y_acc = psum.tile([P, hi - lo], F32, name="y_acc%d" % n, tag="bank%d" % (7, 3, 4, 0, 1)[n])
+            y_acc = psum.tile([P, hi - lo], F32, name="y_acc%d" % n, tag="bank%d" % (7, 3, 1, 0, 4)[n])
             nc.tensor.matmul_mx(
                 y_acc[:],
                 lhsT=w2_codes[:].bitcast(FP4X4),

@@ -87,6 +87,9 @@ def tile_picked_devox_none_p_kernel(
             cols = slice(lo, lo + src.shape[1] // PACK)
             nc.vector.quantize_mx(w1_codes[g][:, cols].bitcast(FP8X4), w1_sc[g][:, cols], src)
 
+        def by_pairs(view):
+            return view.rearrange("p m e j -> p m j e")
+
         def round_w1(hf, g):
             src = raw[hf][g].rearrange("p j (m t) -> p m t j", t=PACK)
             low = staged([P, H], BF16, "low%d_%d" % (hf, g), "low%d_%d" % (hf, g))
@@ -97,11 +100,11 @@ def tile_picked_devox_none_p_kernel(
                 nc.vector.tensor_copy(low_dst, src[:, :, 0:2, :])
                 nc.vector.tensor_copy(high_dst, src[:, :, 2:4, :])
             elif g == 0:
-                nc.scalar.copy(low_dst, src[:, :, 0:2, :])
+                nc.scalar.copy(by_pairs(low_dst), by_pairs(src[:, :, 0:2, :]))
                 nc.gpsimd.tensor_scalar(high_dst, src[:, :, 2:4, :], 1.0, 0.0, MULT, ADD)
             else:
-                nc.scalar.copy(low_dst, src[:, :, 0:2, :])
-                nc.scalar.copy(high_dst, src[:, :, 2:4, :])
+                nc.scalar.copy(by_pairs(low_dst), by_pairs(src[:, :, 0:2, :]))
+                nc.scalar.copy(by_pairs(high_dst), by_pairs(src[:, :, 2:4, :]))
             return low, high
 
         def pack_w1(hf, g, low, high):

@@ -43,12 +43,12 @@ def tile_picked_devox_none_p_kernel(
         xs_mm = keep.tile([P, PASSES, S], U8, name="xs_mm", align_bytes=64)
         nc.gpsimd.memset(xs_all[:].bitcast(I32), 0)
         nc.vector.memset(xs_mm[:].bitcast(I32), 0)
-        up = [keep.tile([P, U], F32, name="up%d" % t) for t in range(2)]
+        up = [keep.tile([P, U], F32, name="up%d" % t) for t in range(3)]
+        up.append(laid.tile([P, U], F32, name="up3", offset=8192, align_bytes=64))
         up_first = keep.tile([P, U], F32, name="up_first")
-        up_second = laid.tile([P, U], F32, name="up_second", offset=8192, align_bytes=64)
         zero = keep.tile([P, 8], F32, name="zero")
         nc.vector.memset(zero[:], 0.0)
-        for window in (up_first, up[0], up_second, up[1]):
+        for window in (up_first, *up):
             nc.scalar.copy(window[:], zero[:, 0:1].to_broadcast([P, U]))
 
         def staged(shape, dtype, name, slot):
@@ -90,46 +90,44 @@ def tile_picked_devox_none_p_kernel(
         def by_pairs(view):
             return view.rearrange("p m e j -> p m j e")
 
-        def round_w1(hf, g):
+        def moves(hf, g, low, high):
             src = raw[hf][g].rearrange("p j (m t) -> p m t j", t=PACK)
-            low = staged([P, H], BF16, "low%d_%d" % (hf, g), "low%d_%d" % (hf, g))
-            high = staged([P, H], BF16, "high%d_%d" % (hf, g), "high%d_%d" % (hf, g))
-            low_dst = low[:].rearrange("p (m e j) -> p m e j", e=2, j=PACK)
-            high_dst = high[:].rearrange("p (e m j) -> p m e j", e=2, j=PACK)
-            if hf == 0:
-                nc.vector.tensor_copy(low_dst, src[:, :, 0:2, :])
-                nc.vector.tensor_copy(high_dst, src[:, :, 2:4, :])
-            elif g == 0:
-                nc.scalar.copy(by_pairs(low_dst), by_pairs(src[:, :, 0:2, :]))
-                nc.gpsimd.tensor_scalar(high_dst, src[:, :, 2:4, :], 1.0, 0.0, MULT, ADD)
-            else:
-                nc.scalar.copy(by_pairs(low_dst), by_pairs(src[:, :, 0:2, :]))
-                nc.scalar.copy(by_pairs(high_dst), by_pairs(src[:, :, 2:4, :]))
+            low_dst = low.rearrange("p (m e j) -> p m e j", e=2, j=PACK)
+            high_dst = high.rearrange("p (e m j) -> p m e j", e=2, j=PACK)
+            return (low_dst, src[:, :, 0:2, :]), (high_dst, src[:, :, 2:4, :])
+
+        def round_w1(g):
+            low = staged([P, H], BF16, "low0_%d" % g, "low0_%d" % g)
+            high = staged([P, H], BF16, "high0_%d" % g, "high0_%d" % g)
+            for move in moves(0, g, low[:], high[:]):
+                nc.vector.tensor_copy(*move)
             return low, high
 
-        def pack_w1(hf, g, low, high):
-            quantize_w1(g, hf * P, low[:])
+        def scalar_round(dst, src):
+            nc.scalar.copy(by_pairs(dst), by_pairs(src))
+
+        def pack_high(hf, g, high):
             for e in range(2):
                 quantize_w1(g, (2 + e) * P + hf * P // 2, high[:, e * H // 2 : (e + 1) * H // 2])
 
-        def prepare_w1(hf, g):
-            pack_w1(hf, g, *round_w1(hf, g))
+        def pack_w1(g, low, high):
+            quantize_w1(g, 0, low[:])
+            pack_high(0, g, high[:])
 
         xs_pick = keep.tile([P, S], U8, name="xs_pick", align_bytes=64)
         xw_pick = [keep.tile([P, S], U32, name="xw_pick%d" % g, align_bytes=64) for g in range(PASSES)]
-        rounded = round_w1(0, 0)
+        rounded = round_w1(0)
         nc.vector.tensor_copy(xs_pick[:], xs_all[:].indirect(offs_sb[:]))
-        up.append(keep.tile([P, U], F32, name="up2"))
-        nc.scalar.copy(up[2][:], zero[:, 0:1].to_broadcast([P, U]))
         for q in (0, 2, 1, 3):
             nc.sync.dma_start(xs_mm[32 * q : 32 * q + 4].bitcast(I32), xs_pick[32 * q : 32 * q + 32 : 4, :].bitcast(I32))
-        pack_w1(0, 0, *rounded)
+        pack_w1(0, *rounded)
         load_w1(1, 0, "low0_0")
-        late = staged([P, S - P + PACK * HALF], F32, "late", "high0_0")
-        raw[1][1] = late[:, S - P :].rearrange("p (j c) -> p j c", j=PACK)
+        EDGE = 8
+        late = staged([P, HALF - PACK * EDGE + PACK * HALF], F32, "late", "high0_0")
+        raw[1][1] = late[:, HALF - PACK * EDGE :].rearrange("p (j c) -> p j c", j=PACK)
         nc.sync.dma_start(raw[1][1], w1_rows[1, 1])
         nc.vector.tensor_copy(xw_pick[0][:], xw_all[0][:].indirect(offs_sb[:]))
-        prepare_w1(0, 1)
+        pack_w1(1, *round_w1(1))
         emb_half = emb.rearrange("(hf m t) c -> hf m t c", hf=2, t=PACK)
         emb_rows = emb.rearrange("(p t) c -> t p c", t=PACK)
         emb_sb = [None] * PACK
@@ -143,9 +141,7 @@ def tile_picked_devox_none_p_kernel(
         for lo, hi in ((0, P), (P, HALF), (HALF, S)):
             nc.vector.tensor_copy(xw_pick[1][:, lo:hi], xw_all[1][:].indirect(offs_sb[:, lo // 16 : hi // 16]))
 
-        h = {t: staged([P, S], F32, "h%d" % t, "h%d" % t) for t in (2, 3)}
-        h[0], h[1] = late[:, 0:S], late[:, S : 2 * S]
-        CUT = 384
+        h = [staged([P, S], F32, "h%d" % t, "h%d" % t) for t in range(PACK)]
 
         def first_product(t, lo, hi, bank, dst):
             acc = psum.tile([P, hi - lo], F32, name="acc%d_%d" % (t, lo), tag="bank%d" % bank)
@@ -167,56 +163,71 @@ def tile_picked_devox_none_p_kernel(
 
         first_product(0, 0, P, 0, h[0][:, 0:P])
         first_product(0, P, HALF, 1, h[0][:, P:HALF])
-        first_product(0, HALF, S - P, 0, h[0][:, HALF : S - P])
         nc.vector.tensor_copy(up_first[:].indirect(cell_sb[:, 0 : P // 16]), h[0][:, 0:P])
         scatter(0, P, HALF, h[0][:, P:HALF])
-        nc.vector.tensor_copy(up_first[:].indirect(cell_sb[:, HALF // 16 : CUT // 16]), h[0][:, HALF:CUT])
-        prepare_w1(1, 0)
-        prepare_w1(1, 1)
-        load_emb(2, "low1_0")
-        load_emb(3, "low0_0")
-        w2_codes = staged([P, 2 * N], U8, "w2_codes", "low1_1")
+        low = staged([P, H], BF16, "low1_0", "low1_0")
+        high = staged([P, H], BF16, "high1_0", "high1_0")
+        low_move, high_move = moves(1, 0, low[:], high[:])
+        scalar_round(*low_move)
+        nc.gpsimd.tensor_scalar(*high_move, 1.0, 0.0, MULT, ADD)
+        quantize_w1(0, P, low[:])
+        pack_high(1, 0, high[:])
+        LOW_AT = H // 2 + PACK * EDGE
+        FRONT = 2 * H - 32
+        shared = keep.tile([P, FRONT + 3 * H], BF16, name="shared", align_bytes=64)
+        stage = shared[:, FRONT : FRONT + LOW_AT + H]
+        low_move, (high_dst, high_src) = moves(1, 1, stage[:, LOW_AT:], stage[:, 0:H])
+        scalar_round(*low_move)
+        scalar_round(high_dst[:, 0:EDGE], high_src[:, 0:EDGE])
+        quantize_w1(1, P, stage[:, LOW_AT:])
+        h_last = late[:, 0:HALF]
+        first_product(0, HALF, S, 0, h_last)
+        scatter(0, HALF, S, h_last)
+        scalar_round(high_dst[:, EDGE:], high_src[:, EDGE:])
+        pack_high(1, 1, stage[:, 0:H])
+        load_emb(2, "low0_0")
+        load_emb(3, "low1_0")
+        w2_codes = staged([P, 2 * N], U8, "w2_codes", "high0_0")
         nc.sync.dma_start(w2_codes[:].bitcast(I32), w2_words[0].bitcast(I32))
-
-        def add_window(dst, window, rows):
-            for quarters in (slice(0, 4, 3), slice(1, 3)):
-                views = [x[:].rearrange("p (k c) -> p k c", c=QUARTER)[:, quarters, :] for x in (dst, window, rows)]
-                nc.gpsimd.tensor_tensor(*views, ADD)
-
-        emb_first = staged([P, U], F32, "emb_first", "high1_1")
-        add_window(emb_first, up_first, emb_sb[0])
-        first_product(0, S - P, S, 1, h[0][:, S - P : S])
-        scatter(0, CUT, S, h[0][:, CUT:S])
         w2_sc = staged([P, N], U8, "w2_sc", "high1_0")
         nc.gpsimd.memset(w2_sc[:].bitcast(I32), 0)
         for q in range(4):
             nc.sync.dma_start(w2_sc[32 * q : 32 * q + 4, :].bitcast(I32), w2_scales[0, 4 * q : 4 * q + 4, :].bitcast(I32))
-        for lo, hi, bank in ((0, P, 3), (P, HALF, 7), (HALF, S, 1)):
+        emb_first = []
+        for quarters, lo in ((slice(0, 4, 3), FRONT + H), (slice(1, 3), 0)):
+            emb_first.append(shared[:, lo : lo + 2 * H].bitcast(F32))
+            views = [x[:].rearrange("p (k c) -> p k c", c=QUARTER)[:, quarters, :] for x in (up_first, emb_sb[0])]
+            nc.gpsimd.tensor_tensor(emb_first[-1].rearrange("p (k c) -> p k c", c=QUARTER), *views, ADD)
+        for lo, hi, bank in ((0, HALF, 3), (HALF, S, 7)):
             first_product(1, lo, hi, bank, h[1][:, lo:hi])
-        nc.vector.tensor_copy(up_second[:].indirect(cell_sb[:, 0 : P // 16]), h[1][:, 0:P])
-        emb_second = keep.tile([P, U], F32, name="emb_second")
-        add_window(emb_second, up_second, emb_sb[1])
-        up.append(placed([P, U], F32, "up3", 8192))
-        nc.gpsimd.memset(up[3][:], 0.0)
-        scatter(1, P, S, h[1][:, P:S])
+        scatter(1, 0, S, h[1][:])
         for t in range(2, PACK):
-            first_product(t, 0, S, (3, 1)[t - 2], h[t][:])
+            first_product(t, 0, S, (3, 7)[t - 2], h[t][:])
             scatter(t, 0, S, h[t][:])
         gate_sb = []
         for d in range(2):
-            gate_sb.append(staged([P, V], F32, "gate_sb%d" % d, "h2" if d == 0 else "raw1"))
+            gate_sb.append(staged([P, V], F32, "gate_sb%d" % d, "h2" if d == 0 else "h1"))
             nc.sync.dma_start(gate_sb[d][:], gate[d])
 
         groups = ((0, 1, 6, 7), (2, 3, 4, 5))
         turned_z = [keep.tile([P, 4, 2 * P], BF16, name="turned_z0"), placed([P, 4, 2 * P], BF16, "turned_z1", 1536)]
-        for s, terms, banks in ((0, (emb_first, up[0]), (0, 4)), (1, (emb_second, up[1]), (3, 1))):
+
+        def blocks(rows, group):
+            return [rows[:, block * P : (block + 1) * P] for block in group]
+
+        for s, banks in ((0, (0, 1)), (1, (3, 7))):
             for b, group in enumerate(groups):
+                if s == 0:
+                    base = blocks(emb_first[b], range(4))
+                else:
+                    base = blocks(emb_sb[1], group)
+                terms = (base, blocks(up[s], group))
                 total = psum.tile([P, 4, P], F32, name="total%d_%d" % (s, b), tag="bank%d" % banks[b])
                 for i, term in enumerate(terms):
-                    for n, block in enumerate(group):
+                    for n in range(4):
                         nc.tensor.matmul(
                             total[:, n, :],
-                            lhsT=term[:, block * P : (block + 1) * P],
+                            lhsT=term[n],
                             rhs=ident[:],
                             is_transpose=True,
                             start=(i == 0 and n == 0),
@@ -259,7 +270,7 @@ def tile_picked_devox_none_p_kernel(
 
         early0 = turn_back(words[0][:, 0:QUARTER], 0, "early0")
         nc.scalar.copy(z_words(z_a[:, 0:P, :])[:, :, 0], early0[:, 0:P])
-        early3 = turn_back(words[0][:, QUARTER : 2 * QUARTER], 4, "early3")
+        early3 = turn_back(words[0][:, QUARTER : 2 * QUARTER], 1, "early3")
         nc.scalar.copy(z_words(z_cd[:, QUARTER:, :])[:, :, 0], early3[:])
         early_mid = {k: turn_back(words[1][:, (k - 1) * QUARTER : k * QUARTER], bank, "early%d" % k) for k, bank in ((2, 5), (1, 2))}
         first_words(0, early0[:, P:QUARTER])
@@ -313,7 +324,7 @@ def tile_picked_devox_none_p_kernel(
             z_codes = placed([P, hi - lo], U32, "z_codes%d" % n, 8192 + 2048 * n)
             z_sc = keep.tile([P, hi - lo], U8, name="z_sc%d" % n, align_bytes=64)
             nc.vector.quantize_mx(z_codes[:].bitcast(FP8X4), z_sc[:], z_bf.rearrange("p c t -> p (c t)"))
-            y_acc = psum.tile([P, hi - lo], F32, name="y_acc%d" % n, tag="bank%d" % (7, 3, 1, 0, 4)[n])
+            y_acc = psum.tile([P, hi - lo], F32, name="y_acc%d" % n, tag="bank%d" % (4, 3, 7, 0, 1)[n])
             nc.tensor.matmul_mx(
                 y_acc[:],
                 lhsT=w2_codes[:].bitcast(FP4X4),

from contextlib import ExitStack

import concourse.mybir as mybir
from concourse.masks import make_identity

K, T, S, V, H, N, U = 1024, 2048, 512, 512, 512, 128, 1024
FLOPS = 2 * K * H * S + 2 * H * N * U

F32 = mybir.dt.float32
BF16 = mybir.dt.bfloat16
I32 = mybir.dt.int32
U32 = mybir.dt.uint32
U16 = mybir.dt.uint16
U8 = mybir.dt.uint8
FP8X4 = mybir.dt.float8_e4m3fn_x4
FP4X4 = mybir.dt.float4_e2m1fn_x4
RELU = mybir.ActivationFunctionType.Relu
ADD = mybir.AluOpType.add
MULT = mybir.AluOpType.mult

P = 128
PACK = 4
PASSES = K // (P * PACK)
HALF = S // 2
QUARTER = U // 4


def tile_picked_devox_none_p_kernel(
    tc, x_words, x_scales, w1, w2_words, w2_scales, gate, emb, offs, cell, pos1, pos2, out
):
    nc = tc.nc
    with ExitStack() as ctx:
        keep = ctx.enter_context(tc.tile_pool(name="keep", bufs=1))
        laid = ctx.enter_context(tc.tile_pool(name="laid", bufs=1))
        psum = ctx.enter_context(tc.psum_pool(name="psum", bufs=1))

        def load_list(src, name):
            tile = keep.tile([P, S // 16], U16, name=name)
            nc.sync.dma_start(tile[:], src)
            return tile

        xs_all = keep.tile([P, T], U8, name="xs_all", align_bytes=64)
        xs_mm = keep.tile([P, PASSES, S], U8, name="xs_mm", align_bytes=64)
        nc.gpsimd.memset(xs_all[:].bitcast(I32), 0)
        nc.vector.memset(xs_mm[:].bitcast(I32), 0)
        up = [keep.tile([P, U], F32, name="up%d" % t) for t in range(3)]
        up.append(laid.tile([P, U], F32, name="up3", offset=8192, align_bytes=64))
        up_first = keep.tile([P, U], F32, name="up_first")
        zero = keep.tile([P, 8], F32, name="zero")
        nc.vector.memset(zero[:], 0.0)
        for window in (up_first, *up):
            nc.scalar.copy(window[:], zero[:, 0:1].to_broadcast([P, U]))

        def staged(shape, dtype, name, slot):
            return keep.tile(shape, dtype, name=name, tag=slot, align_bytes=64)

        def placed(shape, dtype, name, offset):
            return laid.tile(shape, dtype, name=name, offset=offset, align_bytes=64)

        ident = keep.tile([P, P], F32, name="ident")
        make_identity(nc, ident[:])

        w1_rows = w1.rearrange("(g p j) (hf c) -> hf g p j c", p=P, j=PACK, hf=2)
        raw = [[None, None], [None, None]]

        def load_w1(hf, g, slot):
            tile = staged([P, PACK, H // 2], F32, "raw%d_%d" % (hf, g), slot)
            raw[hf][g] = tile[:]
            nc.sync.dma_start(tile[:], w1_rows[hf, g])

        xw_all = [keep.tile([P, T], U32, name="xw_all%d" % g) for g in range(PASSES)]
        x_rows = x_words.rearrange("g p n t -> g p (n t)").bitcast(I32)
        load_w1(0, 0, "raw0")
        offs_sb = load_list(offs, "offs_sb")
        nc.sync.dma_start(xs_all[0:P:4, :].bitcast(I32), x_scales.bitcast(I32).rearrange("g i c -> i g c"))
        cell_sb = load_list(cell, "cell_sb")
        pos_sb = [load_list(pos1, "pos1_sb")]
        nc.sync.dma_start(xw_all[0][:].bitcast(I32), x_rows[0])
        load_w1(0, 1, "raw1")
        nc.sync.dma_start(xw_all[1][:].bitcast(I32), x_rows[1])
        pos_sb.append(load_list(pos2, "pos2_sb"))

        w1_codes = [keep.tile([P, H], U32, name="w1_codes%d" % g, align_bytes=64) for g in range(PASSES)]
        w1_sc = [keep.tile([P, H], U8, name="w1_sc%d" % g, align_bytes=64) for g in range(PASSES)]

        def quantize_w1(g, lo, src):
            cols = slice(lo, lo + src.shape[1] // PACK)
            nc.vector.quantize_mx(w1_codes[g][:, cols].bitcast(FP8X4), w1_sc[g][:, cols], src)

        def by_pairs(view):
            return view.rearrange("p m e j -> p m j e")

        def moves(hf, g, low, high):
            src = raw[hf][g].rearrange("p j (m t) -> p m t j", t=PACK)
            low_dst = low.rearrange("p (m e j) -> p m e j", e=2, j=PACK)
            high_dst = high.rearrange("p (e m j) -> p m e j", e=2, j=PACK)
            return (low_dst, src[:, :, 0:2, :]), (high_dst, src[:, :, 2:4, :])

        def round_w1(g):
            low = staged([P, H], BF16, "low0_%d" % g, "low0_%d" % g)
            high = staged([P, H], BF16, "high0_%d" % g, "high0_%d" % g)
            for move in moves(0, g, low[:], high[:]):
                nc.vector.tensor_copy(*move)
            return low, high

        def scalar_round(dst, src):
            nc.scalar.copy(by_pairs(dst), by_pairs(src))

        def pack_high(hf, g, high):
            for e in range(2):
                quantize_w1(g, (2 + e) * P + hf * P // 2, high[:, e * H // 2 : (e + 1) * H // 2])

        def pack_w1(g, low, high):
            quantize_w1(g, 0, low[:])
            pack_high(0, g, high[:])

        xs_pick = keep.tile([P, S], U8, name="xs_pick", align_bytes=64)
        xw_pick = [keep.tile([P, S], U32, name="xw_pick%d" % g, align_bytes=64) for g in range(PASSES)]
        rounded = round_w1(0)
        nc.vector.tensor_copy(xs_pick[:], xs_all[:].indirect(offs_sb[:]))
        for q in (0, 2, 1, 3):
            nc.sync.dma_start(xs_mm[32 * q : 32 * q + 4].bitcast(I32), xs_pick[32 * q : 32 * q + 32 : 4, :].bitcast(I32))
        pack_w1(0, *rounded)
        load_w1(1, 0, "low0_0")
        EDGE = 8
        late = staged([P, HALF - PACK * EDGE + PACK * HALF], F32, "late", "high0_0")
        raw[1][1] = late[:, HALF - PACK * EDGE :].rearrange("p (j c) -> p j c", j=PACK)
        nc.sync.dma_start(raw[1][1], w1_rows[1, 1])
        nc.vector.tensor_copy(xw_pick[0][:], xw_all[0][:].indirect(offs_sb[:]))
        pack_w1(1, *round_w1(1))
        emb_half = emb.rearrange("(hf m t) c -> hf m t c", hf=2, t=PACK)
        emb_rows = emb.rearrange("(p t) c -> t p c", t=PACK)
        emb_sb = [None] * PACK

        def load_emb(s, slot):
            emb_sb[s] = staged([P, U], F32, "emb_sb%d" % s, slot)
            nc.sync.dma_start(emb_sb[s][:], emb_half[s, :, 0:2, :] if s < 2 else emb_rows[s])

        load_emb(0, "low0_1")
        load_emb(1, "high0_1")
        for lo, hi in ((0, P), (P, HALF), (HALF, S)):
            nc.vector.tensor_copy(xw_pick[1][:, lo:hi], xw_all[1][:].indirect(offs_sb[:, lo // 16 : hi // 16]))

        h = [staged([P, S], F32, "h%d" % t, "h%d" % t) for t in range(PACK)]

        def first_product(t, lo, hi, bank, dst):
            acc = psum.tile([P, hi - lo], F32, name="acc%d_%d" % (t, lo), tag="bank%d" % bank)
            cols = slice(t * P, (t + 1) * P)
            for g in range(PASSES):
                nc.tensor.matmul_mx(
                    acc[:],
                    lhsT=w1_codes[g][:, cols].bitcast(FP8X4),
                    lhsT_scale=w1_sc[g][:, cols],
                    rhs=xw_pick[g][:, lo:hi].bitcast(FP8X4),
                    rhs_scale=xs_mm[:, g, lo:hi],
                    start=(g == 0),
                    stop=(g == PASSES - 1),
                )
            nc.scalar.activation(dst, acc[:], RELU)

        def scatter(t, lo, hi, src):
            nc.vector.tensor_copy(up[t][:].indirect(cell_sb[:, lo // 16 : hi // 16]), src)

        first_product(0, 0, P, 0, h[0][:, 0:P])
        first_product(0, P, HALF, 1, h[0][:, P:HALF])
        nc.vector.tensor_copy(up_first[:].indirect(cell_sb[:, 0 : P // 16]), h[0][:, 0:P])
        scatter(0, P, HALF, h[0][:, P:HALF])
        low = staged([P, H], BF16, "low1_0", "low1_0")
        high = staged([P, H], BF16, "high1_0", "high1_0")
        low_move, high_move = moves(1, 0, low[:], high[:])
        scalar_round(*low_move)
        nc.gpsimd.tensor_scalar(*high_move, 1.0, 0.0, MULT, ADD)
        quantize_w1(0, P, low[:])
        pack_high(1, 0, high[:])
        LOW_AT = H // 2 + PACK * EDGE
        FRONT = 2 * H - 32
        shared = keep.tile([P, FRONT + 3 * H], BF16, name="shared", align_bytes=64)
        stage = shared[:, FRONT : FRONT + LOW_AT + H]
        low_move, (high_dst, high_src) = moves(1, 1, stage[:, LOW_AT:], stage[:, 0:H])
        scalar_round(*low_move)
        scalar_round(high_dst[:, 0:EDGE], high_src[:, 0:EDGE])
        quantize_w1(1, P, stage[:, LOW_AT:])
        h_last = late[:, 0:HALF]
        first_product(0, HALF, S, 0, h_last)
        scatter(0, HALF, S, h_last)
        scalar_round(high_dst[:, EDGE:], high_src[:, EDGE:])
        pack_high(1, 1, stage[:, 0:H])
        load_emb(2, "low0_0")
        load_emb(3, "low1_0")
        w2_codes = staged([P, 2 * N], U8, "w2_codes", "high0_0")
        nc.sync.dma_start(w2_codes[:].bitcast(I32), w2_words[0].bitcast(I32))
        w2_sc = staged([P, N], U8, "w2_sc", "high1_0")
        nc.gpsimd.memset(w2_sc[:].bitcast(I32), 0)
        for q in range(4):
            nc.sync.dma_start(w2_sc[32 * q : 32 * q + 4, :].bitcast(I32), w2_scales[0, 4 * q : 4 * q + 4, :].bitcast(I32))
        emb_first = []
        for quarters, lo in ((slice(0, 4, 3), FRONT + H), (slice(1, 3), 0)):
            emb_first.append(shared[:, lo : lo + 2 * H].bitcast(F32))
            views = [x[:].rearrange("p (k c) -> p k c", c=QUARTER)[:, quarters, :] for x in (up_first, emb_sb[0])]
            nc.gpsimd.tensor_tensor(emb_first[-1].rearrange("p (k c) -> p k c", c=QUARTER), *views, ADD)
        for lo, hi, bank in ((0, HALF, 3), (HALF, S, 7)):
            first_product(1, lo, hi, bank, h[1][:, lo:hi])
        scatter(1, 0, S, h[1][:])
        for t in range(2, PACK):
            first_product(t, 0, S, (3, 7)[t - 2], h[t][:])
            scatter(t, 0, S, h[t][:])
        gate_sb = []
        for d in range(2):
            gate_sb.append(staged([P, V], F32, "gate_sb%d" % d, "h2" if d == 0 else "h1"))
            nc.sync.dma_start(gate_sb[d][:], gate[d])

        groups = ((0, 1, 6, 7), (2, 3, 4, 5))
        turned_z = [keep.tile([P, 4, 2 * P], BF16, name="turned_z0"), placed([P, 4, 2 * P], BF16, "turned_z1", 1536)]

        def blocks(rows, group):
            return [rows[:, block * P : (block + 1) * P] for block in group]

        for s, banks in ((0, (0, 1)), (1, (3, 7))):
            for b, group in enumerate(groups):
                if s == 0:
                    base = blocks(emb_first[b], range(4))
                else:
                    base = blocks(emb_sb[1], group)
                terms = (base, blocks(up[s], group))
                total = psum.tile([P, 4, P], F32, name="total%d_%d" % (s, b), tag="bank%d" % banks[b])
                for i, term in enumerate(terms):
                    for n in range(4):
                        nc.tensor.matmul(
                            total[:, n, :],
                            lhsT=term[n],
                            rhs=ident[:],
                            is_transpose=True,
                            start=(i == 0 and n == 0),
                            stop=(i == len(terms) - 1 and n == 3),
                        )
                nc.scalar.copy(turned_z[b][:, :, s * P : (s + 1) * P], total[:])
        turned_sb = []
        for name, lo, width, bank in (("a", 0, QUARTER, 6), ("m", QUARTER, 2 * QUARTER, 2)):
            turned = psum.tile([P, width], F32, name="turned_" + name, tag="bank%d" % bank)
            for c in range(0, width, P):
                nc.tensor.transpose(turned[:, c : c + P], emb_sb[3][:, lo + c : lo + c + P], ident[:])
            turned_sb.append(keep.tile([P, width], F32, name="turned_sb_" + name))
            nc.scalar.copy(turned_sb[-1][:], turned[:])

        def turn_back(src, bank, name):
            back = psum.tile([P, src.shape[1]], F32, name=name, tag="bank%d" % bank)
            for c in range(0, src.shape[1], P):
                nc.tensor.transpose(back[:, c : c + P], src[:, c : c + P], ident[:])
            return back

        emb_a = turn_back(turned_sb[0][:], 6, "emb_a")
        words = [turned_z[b][:].rearrange("p n h -> p (n h)").bitcast(F32) for b in range(2)]
        z_a = keep.tile([P, QUARTER, PACK], BF16, name="z_a", align_bytes=64)
        z_b = keep.tile([P, QUARTER, PACK], BF16, name="z_b", align_bytes=64)
        z_cd = keep.tile([P, 2 * QUARTER, PACK], BF16, name="z_cd", align_bytes=64)
        DIRECT = 320
        PAIRED = 2 * QUARTER - DIRECT

        def z_words(z):
            return z.rearrange("p c t -> p (c t)").bitcast(F32).rearrange("p (c u) -> p c u", u=2)

        pairs = {
            1: placed([P, 2, QUARTER, 2], BF16, "pairs1", 0),
            2: placed([P, 2, PAIRED, 2], BF16, "pairs2", 3072),
            0: placed([P, 2, P, 2], BF16, "pairs0", 2048),
        }

        def first_words(k, src):
            nc.scalar.copy(pairs[k][:, 0].rearrange("p c e -> p (c e)").bitcast(F32), src)

        early0 = turn_back(words[0][:, 0:QUARTER], 0, "early0")
        nc.scalar.copy(z_words(z_a[:, 0:P, :])[:, :, 0], early0[:, 0:P])
        early3 = turn_back(words[0][:, QUARTER : 2 * QUARTER], 1, "early3")
        nc.scalar.copy(z_words(z_cd[:, QUARTER:, :])[:, :, 0], early3[:])
        early_mid = {k: turn_back(words[1][:, (k - 1) * QUARTER : k * QUARTER], bank, "early%d" % k) for k, bank in ((2, 5), (1, 2))}
        first_words(0, early0[:, P:QUARTER])
        nc.scalar.copy(z_words(z_cd[:, PAIRED:QUARTER, :])[:, :, 0], early_mid[2][:, PAIRED:QUARTER])
        rows = keep.tile([P, 2, P], BF16, name="rows")
        spans = {0: (P, QUARTER), 1: (QUARTER, 2 * QUARTER), 2: (2 * QUARTER, U - DIRECT)}
        middle = keep.tile([P, QUARTER + PAIRED], BF16, name="middle")
        plane2 = {0: rows[:, 1, :], 1: middle[:, 0:QUARTER], 2: middle[:, QUARTER:]}
        nc.gpsimd.tensor_tensor(middle[:], up[2][:, QUARTER : U - DIRECT], emb_sb[2][:, QUARTER : U - DIRECT], ADD)
        nc.gpsimd.tensor_tensor(rows[:].rearrange("p e c -> p (e c)"), up[2][:, 0:QUARTER], emb_sb[2][:, 0:QUARTER], ADD)
        nc.gpsimd.tensor_tensor(z_cd[:, PAIRED:, 2], up[2][:, U - DIRECT : U], emb_sb[2][:, U - DIRECT : U], ADD)
        nc.gpsimd.tensor_tensor(z_cd[:, PAIRED:, 3], up[3][:, U - DIRECT : U], emb_sb[3][:, U - DIRECT : U], ADD)

        first_words(2, early_mid[2][:, 0:PAIRED])
        for k in (1, 2, 0):
            lo, hi = spans[k]
            nc.scalar.copy(pairs[k][:, 1], plane2[k].unsqueeze(2).to_broadcast([P, hi - lo, 2]))
        first_words(1, early_mid[1][:])
        emb_mid = {k: turn_back(turned_sb[1][:, (k - 1) * QUARTER : k * QUARTER], bank, "emb_mid%d" % k) for k, bank in ((2, 5), (1, 2))}
        nc.vector.tensor_tensor(rows[:, 1, :], up[3][:, 0:P], emb_a[:, 0:P], ADD)
        for k, emb_turned in ((0, emb_a[:, P:QUARTER]), (2, emb_mid[2][:, 0:PAIRED]), (1, emb_mid[1][:])):
            lo, hi = spans[k]
            nc.vector.tensor_tensor(pairs[k][:, 1, :, 1], up[3][:, lo:hi], emb_turned, ADD)
        nc.scalar.copy(z_a[:, 0:P, 2:4], rows[:].rearrange("p e c -> p c e"))

        def weave(copy, k, lo, hi, z):
            src = pairs[k][:].rearrange("p u c e -> p u (c e)").bitcast(U32)[:, :, lo:hi]
            dst = z.rearrange("p c t -> p (c t)").bitcast(U32).rearrange("p (c u) -> p c u", u=2)
            if copy is nc.vector:
                copy.tensor_copy(dst.bitcast(I32), src.rearrange("p u c -> p c u").bitcast(I32))
            else:
                copy.copy(dst, src.rearrange("p u c -> p c u"))

        weave(nc.scalar, 0, 0, P, z_a[:, P:QUARTER, :])
        weave(nc.vector, 2, P, PAIRED, z_cd[:, P:PAIRED, :])
        weave(nc.scalar, 2, 0, P, z_cd[:, 0:P, :])
        weave(nc.scalar, 1, 0, P, z_b[:, 0:P, :])
        weave(nc.scalar, 1, P, QUARTER, z_b[:, P:QUARTER, :])
        z_c, z_d = z_cd[:, 0:QUARTER, :], z_cd[:, QUARTER:, :]

        y = keep.tile([P, U], F32, name="y")
        chunks = [
            (z_d, 768, U, nc.scalar.copy),
            (z_a[:], 0, 256, nc.scalar.copy),
            (z_c, 512, 768, nc.vector.tensor_copy),
            (z_b[:, :P, :], 256, 384, nc.vector.tensor_copy),
            (z_b[:, P:, :], 384, 512, nc.scalar.copy),
        ]
        accs = []
        for n, (z_bf, lo, hi, copy) in enumerate(chunks):
            z_codes = placed([P, hi - lo], U32, "z_codes%d" % n, 8192 + 2048 * n)
            z_sc = keep.tile([P, hi - lo], U8, name="z_sc%d" % n, align_bytes=64)
            nc.vector.quantize_mx(z_codes[:].bitcast(FP8X4), z_sc[:], z_bf.rearrange("p c t -> p (c t)"))
            y_acc = psum.tile([P, hi - lo], F32, name="y_acc%d" % n, tag="bank%d" % (4, 3, 7, 0, 1)[n])
            nc.tensor.matmul_mx(
                y_acc[:],
                lhsT=w2_codes[:].bitcast(FP4X4),
                lhsT_scale=w2_sc[:],
                rhs=z_codes[:].bitcast(FP8X4),
                rhs_scale=z_sc[:],
                start=True,
                stop=True,
            )
            accs.append(y_acc)
        for y_acc, (z_bf, lo, hi, copy) in zip(accs, chunks):
            copy(y[:, lo:hi], y_acc[:])

        parts = ((0, 384), (384, V))
        prod = [[keep.tile([P, hi - lo], F32, name="prod%d_%d" % (lo, d)) for d in range(2)] for lo, hi in parts]

        def fetch(a, d):
            lo, hi = parts[a]
            nc.vector.tensor_tensor(prod[a][d][:], y[:].indirect(pos_sb[d][:, lo // 16 : hi // 16]), gate_sb[d][:, lo:hi], MULT)

        def finish(a, lo, hi):
            cols = slice(lo - parts[a][0], hi - parts[a][0])
            res = keep.tile([P, hi - lo], F32, name="res%d" % lo)
            nc.vector.tensor_tensor(res[:], prod[a][0][:, cols], prod[a][1][:, cols], ADD)
            (nc.scalar if hi == V else nc.sync).dma_start(out[:, lo:hi], res[:])

        fetch(0, 0)
        fetch(0, 1)
        fetch(1, 0)
        finish(0, 0, 256)
        fetch(1, 1)
        finish(0, 256, 384)
        finish(1, 384, V)
